import numpy as np
import ml_dtypes


def mxq(x, axis, fmt="e4m3"):
    dtype, down = {"e4m3": (ml_dtypes.float8_e4m3fn, 7), "e5m2": (ml_dtypes.float8_e5m2, 14)}[fmt]
    v = np.moveaxis(np.asarray(x, np.float32).astype(ml_dtypes.bfloat16).astype(np.float64), axis, -1)
    blocks = v.reshape(v.shape[:-1] + (-1, 32))
    amax = np.abs(blocks).max(-1, keepdims=True)
    byte = np.maximum(np.where(amax > 0, np.frexp(amax)[1] - 1 + 127, 0) - down, 1)
    scale = np.exp2(byte - 127.0)
    codes = (blocks / scale).astype(np.float32).astype(dtype).astype(np.float64)
    return np.moveaxis((codes * scale).reshape(v.shape), -1, axis)


WIDE = False


def mx_kscale(k):
    if not WIDE:
        return np.ones(k)
    levels = np.array([10, -10, 5, -5, 0])
    if k % 512:
        return np.exp2(np.random.permutation(np.resize(levels, k // 32))).repeat(32)
    a = np.empty((k // 512, 16))
    for p in range(k // 512):
        a[p, :8] = np.random.permutation(np.resize(levels, 8))
        for g in range(8):
            far = levels[np.abs(levels - a[p, g]) >= 10]
            a[p, g + 8] = far[np.random.randint(len(far))]
    return np.exp2(a.ravel()).repeat(32)


def f64(x):
    return np.asarray(x).astype(np.float64)


def striped(idx):
    return np.tile(idx.reshape(-1, 16).T, (8, 1)).astype(np.uint16)


def unstriped(offs):
    return offs[:16].T.reshape(-1).astype(np.int64)


E2M1 = np.array([0.0, 0.5, 1.0, 1.5, 2.0, 3.0, 4.0, 6.0, -0.0, -0.5, -1.0, -1.5, -2.0, -3.0, -4.0, -6.0])


def pack_fp4(w):
    k, n = w.shape
    w = f64(np.asarray(w, np.float32).astype(ml_dtypes.bfloat16)).reshape(k // 32, 32, n)
    amax = np.abs(w).max(1)
    mant, ex = np.frexp(amax / 6.0)
    byte = np.clip(np.where(amax > 0, np.where(mant > 0.5, ex, ex - 1) + 127, 1), 1, 254)
    scaled = (w * np.exp2(127.0 - byte)[:, None, :]).reshape(k, n).astype(np.float32)
    c = np.ascontiguousarray(scaled.reshape(k // 512, 128, 4, n).transpose(0, 1, 3, 2)).astype(ml_dtypes.float4_e2m1fn).view(np.uint8) & 0xF
    words = (c[..., 0::2] | (c[..., 1::2] << 4)).reshape(k // 512, 128, 2 * n)
    return np.ascontiguousarray(words), np.ascontiguousarray(byte.astype(np.uint8).reshape(k // 512, 16, n))


def unpack_fp4(words, scales):
    g, _, n = scales.shape
    words = np.ascontiguousarray(words).reshape(g, 128, n, 2)
    nib = np.empty((g, 128, n, 4), np.uint8)
    nib[..., 0::2] = words & 0xF
    nib[..., 1::2] = words >> 4
    vals = E2M1[nib] * np.repeat(np.exp2(scales.astype(np.float64) - 127.0), 8, axis=1)[..., None]
    return vals.transpose(0, 1, 3, 2).reshape(g * 512, n)


K, T, S, N, U = 1024, 2048, 1024, 128, 2048


def setup_inputs():
    n = np.random.standard_normal
    s = mx_kscale(K)[:, None]
    packed_w1 = pack_fp4(n((K, N)) / np.sqrt(K) / s)
    return {
        "xT": (n((K, T)) * s).astype(np.float32),
        "mem": n((N, U)).astype(np.float32),
        "w1_words": packed_w1[0],
        "w1_scales": packed_w1[1],
        "offs": striped(np.random.permutation(T)[:S]),
        "slot": striped(np.random.permutation(U)[:S]),
    }


def reference(xT, mem, w1_words, w1_scales, offs, slot):
    xq = mxq(f64(xT)[:, unstriped(offs)], 0, "e4m3")
    y = unpack_fp4(w1_words, w1_scales).T @ xq
    out = f64(mem).copy()
    out[:, unstriped(slot)] = np.maximum(f64(mem)[:, unstriped(slot)], y)
    return out

@@ -1,0 +1,129 @@
+from contextlib import ExitStack
+
+import concourse.mybir as mybir
+
+K, T, S, N, U = 1024, 2048, 1024, 128, 2048
+FLOPS = 2 * K * N * S
+
+F32 = mybir.dt.float32
+BF16 = mybir.dt.bfloat16
+U32 = mybir.dt.uint32
+I32 = mybir.dt.int32
+U16 = mybir.dt.uint16
+U8 = mybir.dt.uint8
+FP8X4 = mybir.dt.float8_e4m3fn_x4
+FP4X4 = mybir.dt.float4_e2m1fn_x4
+
+P = 128
+PASSES = 2
+HALF = 512
+PIECE = 256
+
+LOADS = [
+    [(0, 1024, 1024), (1024, 2048, 1344)],
+    [(0, 1024, 1024), (1024, 2048, 1344)],
+    [(0, 1024, 1024), (1024, 2048, 1344)],
+    [(0, 512, 512), (512, 1024, 1024), (1024, 1536, 1536), (1536, 2048, 1696)],
+]
+
+
+def tile_picked_idxput_max_e_kernel(tc, xT, mem, w1_words, w1_scales, offs, slot, out):
+    nc = tc.nc
+    with ExitStack() as ctx:
+        keep = ctx.enter_context(tc.tile_pool(name="keep", bufs=1))
+        psum = ctx.enter_context(tc.psum_pool(name="psum", bufs=1))
+
+        store = keep.tile([P, U], F32, name="store")
+        slot_sb = keep.tile([P, S // 16], U16, name="slot_sb")
+        offs_sb = keep.tile([P, S // 16], U16, name="offs_sb")
+        w_words = keep.tile([P, PASSES, 2 * N], U8, name="w_words", align_bytes=64)
+        w_scales = keep.tile([P, PASSES, N], U8, name="w_scales", align_bytes=64)
+
+        x_rows = xT.rearrange("(g p u e) t -> g u p e t", g=PASSES, p=P, u=2, e=2)
+        raw = {}
+
+        def load(pair, c):
+            c0, c1, split = LOADS[pair][c]
+            raw[pair, c] = keep.tile([P, 2, c1 - c0], F32, name="raw_%d_%d" % (pair, c))
+            nc.sync.dma_start(out=raw[pair, c][:], in_=x_rows[pair // 2, pair % 2][:, :, c0:c1])
+
+        load(0, 0)
+        nc.sync.dma_start(offs_sb[:], offs)
+        load(0, 1)
+        for pair in range(1, 4):
+            for c in range(len(LOADS[pair])):
+                load(pair, c)
+        nc.sync.dma_start(out=store[:], in_=mem)
+        nc.sync.dma_start(slot_sb[:], slot)
+
+        nc.gpsimd.memset(w_scales[:].rearrange("p g n -> p (g n)"), 0)
+        nc.gpsimd.dma_start(out=w_words[:].bitcast(I32), in_=w1_words.rearrange("g p n -> p g n").bitcast(I32))
+        for q in range(4):
+            nc.gpsimd.dma_start(
+                out=w_scales[32 * q : 32 * q + 4, :, :].bitcast(I32),
+                in_=w1_scales[:, 4 * q : 4 * q + 4, :].rearrange("g r n -> r g n").bitcast(I32),
+            )
+
+        old = keep.tile([P, S], F32, name="old")
+
+        pairs = [keep.tile([P, T, 2], BF16, name="pairs_%d" % i) for i in range(4)]
+        picked = keep.tile([P, S // PIECE, 2, PIECE], U32, name="picked")
+        woven = [keep.tile([P, S, 2], U32, name="woven_%d" % g, align_bytes=64) for g in range(PASSES)]
+        codes = [keep.tile([P, S], U32, name="codes_%d" % g, align_bytes=64) for g in range(PASSES)]
+        scales = [keep.tile([P, S], U8, name="scales_%d" % g, align_bytes=64) for g in range(PASSES)]
+        acc = [psum.tile([P, HALF], F32, name="acc_%d" % h) for h in range(2)]
+        new = keep.tile([P, S], F32, name="new")
+
+        def cast(pair):
+            for c, (c0, c1, split) in enumerate(LOADS[pair]):
+                src = raw[pair, c][:].rearrange("p e t -> p t e")
+                nc.scalar.copy(out=pairs[pair][:, c0:split, :], in_=src[:, : split - c0, :])
+                if split < c1:
+                    nc.vector.tensor_copy(out=pairs[pair][:, split:c1, :], in_=src[:, split - c0 :, :])
+
+        def gather(pair, j0, j1, dst):
+            window = pairs[pair][:].rearrange("p t e -> p (t e)").bitcast(U32)
+            nc.vector.tensor_copy(dst, window.indirect(offs_sb[:, j0 // 16 : j1 // 16]))
+
+        def quantise(g, j0, j1):
+            nc.vector.quantize_mx(
+                out=codes[g][:, j0:j1].bitcast(FP8X4),
+                scales=scales[g][:, j0:j1],
+                in_=woven[g][:, j0:j1, :].rearrange("p s u -> p (s u)").bitcast(BF16),
+            )
+
+        def multiply(g, h):
+            cols = slice(h * HALF, (h + 1) * HALF)
+            nc.tensor.matmul_mx(
+                out=acc[h][:],
+                lhsT=w_words[:, g, :].bitcast(FP4X4),
+                lhsT_scale=w_scales[:, g, :],
+                rhs=codes[g][:, cols].bitcast(FP8X4),
+                rhs_scale=scales[g][:, cols],
+                start=(g == 0),
+                stop=(g == PASSES - 1),
+            )
+
+        cast(0)
+        gather(0, 0, S, woven[0][:, :, 0])
+        cast(1)
+        gather(1, 0, S, woven[0][:, :, 1])
+        cast(2)
+        gather(2, 0, S, picked[:, :, 0, :])
+        quantise(0, 0, S)
+        for h in range(2):
+            multiply(0, h)
+        cast(3)
+        for i in range(S // PIECE):
+            j0 = i * PIECE
+            gather(3, j0, j0 + PIECE, picked[:, i, 1, :])
+            nc.scalar.copy(out=woven[1][:, j0 : j0 + PIECE, :], in_=picked[:, i, :, :].rearrange("p u s -> p s u"))
+        for h in range(2):
+            quantise(1, h * HALF, (h + 1) * HALF)
+            multiply(1, h)
+            nc.vector.tensor_copy(old[:, h * HALF : (h + 1) * HALF], store[:].indirect(slot_sb[:, h * HALF // 16 : (h + 1) * HALF // 16]))
+        for h in range(2):
+            cols = slice(h * HALF, (h + 1) * HALF)
+            nc.vector.tensor_tensor(out=new[:, cols], in0=acc[h][:], in1=old[:, cols], op=mybir.AluOpType.max)
+        nc.vector.tensor_copy(store[:].indirect(slot_sb[:]), new[:])
+        nc.sync.dma_start(out=out, in_=store[:])

@@ -22,7 +22,7 @@ PIECE = 256
 LOADS = [
     [(0, 1024, 1024), (1024, 2048, 1344)],
     [(0, 1024, 1024), (1024, 2048, 1344)],
-    [(0, 1024, 1024), (1024, 2048, 1344)],
+    [(0, 1024, 1024), (1024, 2048, 1664)],
     [(0, 512, 512), (512, 1024, 1024), (1024, 1536, 1536), (1536, 2048, 1696)],
 ]
 
@@ -77,7 +77,8 @@ def tile_picked_idxput_max_e_kernel(tc, xT, mem, w1_words, w1_scales, offs, slot
         def cast(pair):
             for c, (c0, c1, split) in enumerate(LOADS[pair]):
                 src = raw[pair, c][:].rearrange("p e t -> p t e")
-                nc.scalar.copy(out=pairs[pair][:, c0:split, :], in_=src[:, : split - c0, :])
+                if split > c0:
+                    nc.scalar.copy(out=pairs[pair][:, c0:split, :], in_=src[:, : split - c0, :])
                 if split < c1:
                     nc.vector.tensor_copy(out=pairs[pair][:, split:c1, :], in_=src[:, split - c0 :, :])
 
@@ -108,16 +109,18 @@ def tile_picked_idxput_max_e_kernel(tc, xT, mem, w1_words, w1_scales, offs, slot
         gather(0, 0, S, woven[0][:, :, 0])
         cast(1)
         gather(1, 0, S, woven[0][:, :, 1])
-        cast(2)
-        gather(2, 0, S, picked[:, :, 0, :])
         quantise(0, 0, S)
         for h in range(2):
             multiply(0, h)
+        cast(2)
+        gather(2, 0, S, picked[:, :, 0, :])
         cast(3)
-        for i in range(S // PIECE):
-            j0 = i * PIECE
-            gather(3, j0, j0 + PIECE, picked[:, i, 1, :])
-            nc.scalar.copy(out=woven[1][:, j0 : j0 + PIECE, :], in_=picked[:, i, :, :].rearrange("p u s -> p s u"))
+        for i0, i1 in ((0, 1), (1, 2), (2, 4)):
+            gather(3, i0 * PIECE, i1 * PIECE, picked[:, i0:i1, 1, :])
+            nc.scalar.copy(
+                out=woven[1][:, i0 * PIECE : i1 * PIECE, :].rearrange("p (i s) u -> p i s u", s=PIECE),
+                in_=picked[:, i0:i1, :, :].rearrange("p i u s -> p i s u"),
+            )
         for h in range(2):
             quantise(1, h * HALF, (h + 1) * HALF)
             multiply(1, h)

@@ -22,7 +22,7 @@ PIECE = 256
 LOADS = [
     [(0, 1024, 1024), (1024, 2048, 1344)],
     [(0, 1024, 1024), (1024, 2048, 1344)],
-    [(0, 1024, 1024), (1024, 2048, 1664)],
+    [(0, 1024, 1024), (1024, 2048, 1536)],
     [(0, 512, 512), (512, 1024, 1024), (1024, 1536, 1536), (1536, 2048, 1696)],
 ]
 
@@ -57,17 +57,16 @@ def tile_picked_idxput_max_e_kernel(tc, xT, mem, w1_words, w1_scales, offs, slot
         nc.sync.dma_start(slot_sb[:], slot)
 
         nc.gpsimd.memset(w_scales[:].rearrange("p g n -> p (g n)"), 0)
-        nc.gpsimd.dma_start(out=w_words[:].bitcast(I32), in_=w1_words.rearrange("g p n -> p g n").bitcast(I32))
+        nc.sync.dma_start(out=w_words[:].bitcast(I32), in_=w1_words.rearrange("g p n -> p g n").bitcast(I32))
         for q in range(4):
-            nc.gpsimd.dma_start(
+            nc.sync.dma_start(
                 out=w_scales[32 * q : 32 * q + 4, :, :].bitcast(I32),
                 in_=w1_scales[:, 4 * q : 4 * q + 4, :].rearrange("g r n -> r g n").bitcast(I32),
             )
 
-        old = keep.tile([P, S], F32, name="old")
 
         pairs = [keep.tile([P, T, 2], BF16, name="pairs_%d" % i) for i in range(4)]
-        picked = keep.tile([P, S // PIECE, 2, PIECE], U32, name="picked")
+        picked = keep.tile([P, S // PIECE, 2, PIECE], U32, name="picked", tag="picked")
         woven = [keep.tile([P, S, 2], U32, name="woven_%d" % g, align_bytes=64) for g in range(PASSES)]
         codes = [keep.tile([P, S], U32, name="codes_%d" % g, align_bytes=64) for g in range(PASSES)]
         scales = [keep.tile([P, S], U8, name="scales_%d" % g, align_bytes=64) for g in range(PASSES)]
@@ -121,12 +120,13 @@ def tile_picked_idxput_max_e_kernel(tc, xT, mem, w1_words, w1_scales, offs, slot
                 out=woven[1][:, i0 * PIECE : i1 * PIECE, :].rearrange("p (i s) u -> p i s u", s=PIECE),
                 in_=picked[:, i0:i1, :, :].rearrange("p i u s -> p i s u"),
             )
+        old = [keep.tile([P, HALF], F32, name="old_0"), keep.tile([P, HALF], F32, name="old_1", tag="picked")]
         for h in range(2):
             quantise(1, h * HALF, (h + 1) * HALF)
             multiply(1, h)
-            nc.vector.tensor_copy(old[:, h * HALF : (h + 1) * HALF], store[:].indirect(slot_sb[:, h * HALF // 16 : (h + 1) * HALF // 16]))
+            nc.vector.tensor_copy(old[h][:], store[:].indirect(slot_sb[:, h * HALF // 16 : (h + 1) * HALF // 16]))
         for h in range(2):
             cols = slice(h * HALF, (h + 1) * HALF)
-            nc.vector.tensor_tensor(out=new[:, cols], in0=acc[h][:], in1=old[:, cols], op=mybir.AluOpType.max)
+            nc.vector.tensor_tensor(out=new[:, cols], in0=acc[h][:], in1=old[h][:], op=mybir.AluOpType.max)
         nc.vector.tensor_copy(store[:].indirect(slot_sb[:]), new[:])
         nc.sync.dma_start(out=out, in_=store[:])

@@ -13,18 +13,18 @@ U16 = mybir.dt.uint16
 U8 = mybir.dt.uint8
 FP8X4 = mybir.dt.float8_e4m3fn_x4
 FP4X4 = mybir.dt.float4_e2m1fn_x4
+COPY = mybir.ActivationFunctionType.Copy
 
 P = 128
 PASSES = 2
-HALF = 512
-PIECE = 256
 
 LOADS = [
     [(0, 1024, 1024), (1024, 2048, 1344)],
-    [(0, 1024, 1024), (1024, 2048, 1344)],
-    [(0, 1024, 1024), (1024, 2048, 1536)],
-    [(0, 512, 512), (512, 1024, 1024), (1024, 1536, 1536), (1536, 2048, 1696)],
+    [(0, 1024, 1024), (1024, 1536, 1024), (1536, 2048, 1696)],
+    [(0, 1024, 1024), (1024, 1536, 1280), (1536, 2048, 1696)],
 ]
+PLANE_LOADS = [[(0, 1024), (1024, 2048)], [(0, 1024), (1024, 2048)]]
+RUNS = [(0, 256), (256, 512), (512, 1024)]
 
 
 def tile_picked_idxput_max_e_kernel(tc, xT, mem, w1_words, w1_scales, offs, slot, out):
@@ -41,20 +41,28 @@ def tile_picked_idxput_max_e_kernel(tc, xT, mem, w1_words, w1_scales, offs, slot
 
         x_rows = xT.rearrange("(g p u e) t -> g u p e t", g=PASSES, p=P, u=2, e=2)
         raw = {}
+        plane = [keep.tile([P, T], F32, name="plane_%d" % e) for e in range(2)]
 
         def load(pair, c):
             c0, c1, split = LOADS[pair][c]
             raw[pair, c] = keep.tile([P, 2, c1 - c0], F32, name="raw_%d_%d" % (pair, c))
             nc.sync.dma_start(out=raw[pair, c][:], in_=x_rows[pair // 2, pair % 2][:, :, c0:c1])
 
+        def load_plane(e):
+            for c0, c1 in PLANE_LOADS[e]:
+                nc.sync.dma_start(out=plane[e][:, c0:c1], in_=x_rows[1, 1][:, e, c0:c1])
+
         load(0, 0)
         nc.sync.dma_start(offs_sb[:], offs)
-        load(0, 1)
-        for pair in range(1, 4):
+        for c in range(1, len(LOADS[0])):
+            load(0, c)
+        for pair in range(1, 3):
             for c in range(len(LOADS[pair])):
                 load(pair, c)
-        nc.sync.dma_start(out=store[:], in_=mem)
+        load_plane(0)
+        load_plane(1)
         nc.sync.dma_start(slot_sb[:], slot)
+        nc.sync.dma_start(out=store[:], in_=mem)
 
         nc.gpsimd.memset(w_scales[:].rearrange("p g n -> p (g n)"), 0)
         nc.sync.dma_start(out=w_words[:].bitcast(I32), in_=w1_words.rearrange("g p n -> p g n").bitcast(I32))
@@ -64,14 +72,15 @@ def tile_picked_idxput_max_e_kernel(tc, xT, mem, w1_words, w1_scales, offs, slot
                 in_=w1_scales[:, 4 * q : 4 * q + 4, :].rearrange("g r n -> r g n").bitcast(I32),
             )
 
-
-        pairs = [keep.tile([P, T, 2], BF16, name="pairs_%d" % i) for i in range(4)]
-        picked = keep.tile([P, S // PIECE, 2, PIECE], U32, name="picked", tag="picked")
-        woven = [keep.tile([P, S, 2], U32, name="woven_%d" % g, align_bytes=64) for g in range(PASSES)]
-        codes = [keep.tile([P, S], U32, name="codes_%d" % g, align_bytes=64) for g in range(PASSES)]
-        scales = [keep.tile([P, S], U8, name="scales_%d" % g, align_bytes=64) for g in range(PASSES)]
-        acc = [psum.tile([P, HALF], F32, name="acc_%d" % h) for h in range(2)]
-        new = keep.tile([P, S], F32, name="new")
+        width = [j1 - j0 for j0, j1 in RUNS]
+        pairs = [keep.tile([P, T, 2], BF16, name="pairs_%d" % i) for i in range(3)]
+        rounded = [keep.tile([P, T], BF16, name="rounded_%d" % e) for e in range(2)]
+        woven0 = keep.tile([P, S, 2], U32, name="woven0", align_bytes=64)
+        woven1 = [keep.tile([P, width[r], 2], U32, name="woven1_%d" % r, align_bytes=64) for r in range(len(RUNS))]
+        codes0 = keep.tile([P, S], U32, name="codes0", align_bytes=64)
+        scales0 = keep.tile([P, S], U8, name="scales0", align_bytes=64)
+        acc = [psum.tile([P, width[r]], F32, name="acc_%d" % r) for r in range(len(RUNS))]
+        codes1, scales1, old, new = {}, {}, {}, {}
 
         def cast(pair):
             for c, (c0, c1, split) in enumerate(LOADS[pair]):
@@ -81,52 +90,94 @@ def tile_picked_idxput_max_e_kernel(tc, xT, mem, w1_words, w1_scales, offs, slot
                 if split < c1:
                     nc.vector.tensor_copy(out=pairs[pair][:, split:c1, :], in_=src[:, split - c0 :, :])
 
+        def entries(lst, j0, j1):
+            return lst[:, j0 // 16 : j1 // 16]
+
         def gather(pair, j0, j1, dst):
             window = pairs[pair][:].rearrange("p t e -> p (t e)").bitcast(U32)
-            nc.vector.tensor_copy(dst, window.indirect(offs_sb[:, j0 // 16 : j1 // 16]))
+            nc.vector.tensor_copy(dst, window.indirect(entries(offs_sb, j0, j1)))
 
-        def quantise(g, j0, j1):
-            nc.vector.quantize_mx(
-                out=codes[g][:, j0:j1].bitcast(FP8X4),
-                scales=scales[g][:, j0:j1],
-                in_=woven[g][:, j0:j1, :].rearrange("p s u -> p (s u)").bitcast(BF16),
-            )
+        def as_bf16(words):
+            return words.rearrange("p s u -> p (s u)").bitcast(BF16)
 
-        def multiply(g, h):
-            cols = slice(h * HALF, (h + 1) * HALF)
-            nc.tensor.matmul_mx(
-                out=acc[h][:],
-                lhsT=w_words[:, g, :].bitcast(FP4X4),
-                lhsT_scale=w_scales[:, g, :],
-                rhs=codes[g][:, cols].bitcast(FP8X4),
-                rhs_scale=scales[g][:, cols],
-                start=(g == 0),
-                stop=(g == PASSES - 1),
-            )
+        def round_plane(e):
+            for c0, c1 in PLANE_LOADS[e]:
+                nc.scalar.copy(out=rounded[e][:, c0:c1], in_=plane[e][:, c0:c1])
+
+        def gather_on_vector(e):
+            four = as_bf16(woven1[0][:]).rearrange("p (s t) -> p s t", t=4)
+            nc.vector.tensor_copy(four[:, :, 2 + e], plane[e][:].indirect(entries(offs_sb, *RUNS[0])))
+
+        def gather_on_scalar(e, r):
+            four = as_bf16(woven1[r][:]).rearrange("p (s t) -> p s t", t=4)
+            nc.scalar.activation(four[:, :, 2 + e], rounded[e][:].indirect(entries(offs_sb, *RUNS[r])), COPY)
+
+        def quantise0(j0, j1):
+            nc.vector.quantize_mx(out=codes0[:, j0:j1].bitcast(FP8X4), scales=scales0[:, j0:j1], in_=as_bf16(woven0[:, j0:j1, :]))
+
+        def quantise1(r, tag):
+            codes1[r] = keep.tile([P, width[r]], U32, name="codes1_%d" % r, tag=tag, align_bytes=64)
+            scales1[r] = keep.tile([P, width[r]], U8, name="scales1_%d" % r, align_bytes=64)
+            nc.vector.quantize_mx(out=codes1[r][:].bitcast(FP8X4), scales=scales1[r][:], in_=as_bf16(woven1[r][:]))
+
+        def multiply(r):
+            n = 512 if width[r] == 512 else 128
+            for c0 in range(0, width[r], n):
+                first = slice(RUNS[r][0] + c0, RUNS[r][0] + c0 + n)
+                second = slice(c0, c0 + n)
+                for g, (words, plane_of_scales) in enumerate(((codes0[:, first], scales0[:, first]), (codes1[r][:, second], scales1[r][:, second]))):
+                    nc.tensor.matmul_mx(
+                        out=acc[r][:, second],
+                        lhsT=w_words[:, g, :].bitcast(FP4X4),
+                        lhsT_scale=w_scales[:, g, :],
+                        rhs=words.bitcast(FP8X4),
+                        rhs_scale=plane_of_scales,
+                        start=(g == 0),
+                        stop=(g == PASSES - 1),
+                    )
+
+        def look_up(r, tag):
+            old[r] = keep.tile([P, width[r]], F32, name="old_%d" % r, tag=tag, align_bytes=64)
+            nc.vector.tensor_copy(old[r][:], store[:].indirect(entries(slot_sb, *RUNS[r])))
+
+        def larger(r, tag):
+            new[r] = keep.tile([P, width[r]], F32, name="new_%d" % r, tag=tag, align_bytes=64)
+            nc.vector.tensor_tensor(out=new[r][:], in0=acc[r][:], in1=old[r][:], op=mybir.AluOpType.max)
+
+        def put(r):
+            nc.vector.tensor_copy(store[:].indirect(entries(slot_sb, *RUNS[r])), new[r][:])
 
         cast(0)
-        gather(0, 0, S, woven[0][:, :, 0])
+        gather(0, 0, S, woven0[:, :, 0])
         cast(1)
-        gather(1, 0, S, woven[0][:, :, 1])
-        quantise(0, 0, S)
-        for h in range(2):
-            multiply(0, h)
+        for j0 in (0, 512):
+            gather(1, j0, j0 + 512, woven0[:, j0 : j0 + 512, 1])
+        for j0 in (0, 512):
+            quantise0(j0, j0 + 512)
         cast(2)
-        gather(2, 0, S, picked[:, :, 0, :])
-        cast(3)
-        for i0, i1 in ((0, 1), (1, 2), (2, 4)):
-            gather(3, i0 * PIECE, i1 * PIECE, picked[:, i0:i1, 1, :])
-            nc.scalar.copy(
-                out=woven[1][:, i0 * PIECE : i1 * PIECE, :].rearrange("p (i s) u -> p i s u", s=PIECE),
-                in_=picked[:, i0:i1, :, :].rearrange("p i u s -> p i s u"),
-            )
-        old = [keep.tile([P, HALF], F32, name="old_0"), keep.tile([P, HALF], F32, name="old_1", tag="picked")]
-        for h in range(2):
-            quantise(1, h * HALF, (h + 1) * HALF)
-            multiply(1, h)
-            nc.vector.tensor_copy(old[h][:], store[:].indirect(slot_sb[:, h * HALF // 16 : (h + 1) * HALF // 16]))
-        for h in range(2):
-            cols = slice(h * HALF, (h + 1) * HALF)
-            nc.vector.tensor_tensor(out=new[:, cols], in0=acc[h][:], in1=old[h][:], op=mybir.AluOpType.max)
-        nc.vector.tensor_copy(store[:].indirect(slot_sb[:]), new[:])
+        for r in range(len(RUNS)):
+            gather(2, *RUNS[r], woven1[r][:, :, 0])
+        round_plane(0)
+        gather_on_vector(0)
+        for r in (1, 2):
+            gather_on_scalar(0, r)
+        round_plane(1)
+        gather_on_vector(1)
+        for r in (1, 2):
+            gather_on_scalar(1, r)
+        quantise1(0, "codes1_0")
+        multiply(0)
+        look_up(0, "old_0")
+        look_up(1, "old_1")
+        larger(0, "new_0")
+        look_up(2, "old_2")
+        quantise1(1, "old_0")
+        multiply(1)
+        put(0)
+        larger(1, "new_1")
+        quantise1(2, "old_1")
+        multiply(2)
+        put(1)
+        larger(2, "new_2")
+        put(2)
         nc.sync.dma_start(out=out, in_=store[:])

@@ -20,10 +20,11 @@ PASSES = 2
 
 LOADS = [
     [(0, 1024, 1024), (1024, 2048, 1344)],
-    [(0, 1024, 1024), (1024, 1536, 1024), (1536, 2048, 1696)],
-    [(0, 1024, 1024), (1024, 1536, 1280), (1536, 2048, 1696)],
+    [(0, 512, 512), (512, 1024, 1024), (1024, 1536, 1536), (1536, 2048, 1696)],
+    [(0, 512, 512), (512, 1024, 1024), (1024, 1536, 1536), (1536, 2048, 2048)],
 ]
-PLANE_LOADS = [[(0, 1024), (1024, 2048)], [(0, 1024), (1024, 2048)]]
+PLANE_LOADS = [[(0, 1024), (1024, 2048)], [(0, 2048)]]
+WOVEN = (2,)
 RUNS = [(0, 256), (256, 512), (512, 1024)]
 
 
@@ -75,12 +76,14 @@ def tile_picked_idxput_max_e_kernel(tc, xT, mem, w1_words, w1_scales, offs, slot
         width = [j1 - j0 for j0, j1 in RUNS]
         pairs = [keep.tile([P, T, 2], BF16, name="pairs_%d" % i) for i in range(3)]
         rounded = [keep.tile([P, T], BF16, name="rounded_%d" % e) for e in range(2)]
+        picked = {r: keep.tile([P, 2, width[r]], U32, name="picked_%d" % r) for r in WOVEN}
         woven0 = keep.tile([P, S, 2], U32, name="woven0", align_bytes=64)
         woven1 = [keep.tile([P, width[r], 2], U32, name="woven1_%d" % r, align_bytes=64) for r in range(len(RUNS))]
         codes0 = keep.tile([P, S], U32, name="codes0", align_bytes=64)
         scales0 = keep.tile([P, S], U8, name="scales0", align_bytes=64)
         acc = [psum.tile([P, width[r]], F32, name="acc_%d" % r) for r in range(len(RUNS))]
-        codes1, scales1, old, new = {}, {}, {}, {}
+        old = keep.tile([P, S], F32, name="old")
+        codes1, scales1, new = {}, {}, {}
 
         def cast(pair):
             for c, (c0, c1, split) in enumerate(LOADS[pair]):
@@ -109,8 +112,14 @@ def tile_picked_idxput_max_e_kernel(tc, xT, mem, w1_words, w1_scales, offs, slot
             nc.vector.tensor_copy(four[:, :, 2 + e], plane[e][:].indirect(entries(offs_sb, *RUNS[0])))
 
         def gather_on_scalar(e, r):
-            four = as_bf16(woven1[r][:]).rearrange("p (s t) -> p s t", t=4)
-            nc.scalar.activation(four[:, :, 2 + e], rounded[e][:].indirect(entries(offs_sb, *RUNS[r])), COPY)
+            if r in WOVEN:
+                dst = picked[r][:, 1, :].bitcast(BF16).rearrange("p (s e) -> p s e", e=2)[:, :, e]
+            else:
+                dst = as_bf16(woven1[r][:]).rearrange("p (s t) -> p s t", t=4)[:, :, 2 + e]
+            nc.scalar.activation(dst, rounded[e][:].indirect(entries(offs_sb, *RUNS[r])), COPY)
+
+        def weave(r):
+            nc.scalar.copy(out=woven1[r][:], in_=picked[r][:].rearrange("p u s -> p s u"))
 
         def quantise0(j0, j1):
             nc.vector.quantize_mx(out=codes0[:, j0:j1].bitcast(FP8X4), scales=scales0[:, j0:j1], in_=as_bf16(woven0[:, j0:j1, :]))
@@ -136,13 +145,9 @@ def tile_picked_idxput_max_e_kernel(tc, xT, mem, w1_words, w1_scales, offs, slot
                         stop=(g == PASSES - 1),
                     )
 
-        def look_up(r, tag):
-            old[r] = keep.tile([P, width[r]], F32, name="old_%d" % r, tag=tag, align_bytes=64)
-            nc.vector.tensor_copy(old[r][:], store[:].indirect(entries(slot_sb, *RUNS[r])))
-
         def larger(r, tag):
             new[r] = keep.tile([P, width[r]], F32, name="new_%d" % r, tag=tag, align_bytes=64)
-            nc.vector.tensor_tensor(out=new[r][:], in0=acc[r][:], in1=old[r][:], op=mybir.AluOpType.max)
+            nc.vector.tensor_tensor(out=new[r][:], in0=acc[r][:], in1=old[:, RUNS[r][0] : RUNS[r][1]], op=mybir.AluOpType.max)
 
         def put(r):
             nc.vector.tensor_copy(store[:].indirect(entries(slot_sb, *RUNS[r])), new[r][:])
@@ -156,7 +161,7 @@ def tile_picked_idxput_max_e_kernel(tc, xT, mem, w1_words, w1_scales, offs, slot
             quantise0(j0, j0 + 512)
         cast(2)
         for r in range(len(RUNS)):
-            gather(2, *RUNS[r], woven1[r][:, :, 0])
+            gather(2, *RUNS[r], picked[r][:, 0, :] if r in WOVEN else woven1[r][:, :, 0])
         round_plane(0)
         gather_on_vector(0)
         for r in (1, 2):
@@ -165,17 +170,16 @@ def tile_picked_idxput_max_e_kernel(tc, xT, mem, w1_words, w1_scales, offs, slot
         gather_on_vector(1)
         for r in (1, 2):
             gather_on_scalar(1, r)
-        quantise1(0, "codes1_0")
+        weave(2)
+        quantise1(0, "codes1")
         multiply(0)
-        look_up(0, "old_0")
-        look_up(1, "old_1")
+        nc.vector.tensor_copy(old[:], store[:].indirect(slot_sb[:]))
         larger(0, "new_0")
-        look_up(2, "old_2")
-        quantise1(1, "old_0")
+        quantise1(1, "codes1")
         multiply(1)
         put(0)
         larger(1, "new_1")
-        quantise1(2, "old_1")
+        quantise1(2, "codes1")
         multiply(2)
         put(1)
         larger(2, "new_2")

@@ -23,7 +23,7 @@ LOADS = [
     [(0, 512, 512), (512, 1024, 1024), (1024, 1536, 1536), (1536, 2048, 1696)],
     [(0, 512, 512), (512, 1024, 1024), (1024, 1536, 1536), (1536, 2048, 2048)],
 ]
-PLANE_LOADS = [[(0, 1024), (1024, 2048)], [(0, 2048)]]
+PLANE_LOADS = [[(0, 1024), (1024, 2048)], [(0, 1024), (1024, 2048)]]
 WOVEN = (2,)
 RUNS = [(0, 256), (256, 512), (512, 1024)]
 
@@ -42,7 +42,7 @@ def tile_picked_idxput_max_e_kernel(tc, xT, mem, w1_words, w1_scales, offs, slot
 
         x_rows = xT.rearrange("(g p u e) t -> g u p e t", g=PASSES, p=P, u=2, e=2)
         raw = {}
-        plane = [keep.tile([P, T], F32, name="plane_%d" % e) for e in range(2)]
+        plane = [keep.tile([P, T], F32, name="plane_%d" % e, tag="plane_%d" % e, align_bytes=64) for e in range(2)]
 
         def load(pair, c):
             c0, c1, split = LOADS[pair][c]
@@ -61,9 +61,9 @@ def tile_picked_idxput_max_e_kernel(tc, xT, mem, w1_words, w1_scales, offs, slot
             for c in range(len(LOADS[pair])):
                 load(pair, c)
         load_plane(0)
-        load_plane(1)
         nc.sync.dma_start(slot_sb[:], slot)
         nc.sync.dma_start(out=store[:], in_=mem)
+        load_plane(1)
 
         nc.gpsimd.memset(w_scales[:].rearrange("p g n -> p (g n)"), 0)
         nc.sync.dma_start(out=w_words[:].bitcast(I32), in_=w1_words.rearrange("g p n -> p g n").bitcast(I32))
@@ -82,8 +82,7 @@ def tile_picked_idxput_max_e_kernel(tc, xT, mem, w1_words, w1_scales, offs, slot
         codes0 = keep.tile([P, S], U32, name="codes0", align_bytes=64)
         scales0 = keep.tile([P, S], U8, name="scales0", align_bytes=64)
         acc = [psum.tile([P, width[r]], F32, name="acc_%d" % r) for r in range(len(RUNS))]
-        old = keep.tile([P, S], F32, name="old")
-        codes1, scales1, new = {}, {}, {}
+        codes1, scales1, old, new = {}, {}, {}, {}
 
         def cast(pair):
             for c, (c0, c1, split) in enumerate(LOADS[pair]):
@@ -145,9 +144,13 @@ def tile_picked_idxput_max_e_kernel(tc, xT, mem, w1_words, w1_scales, offs, slot
                         stop=(g == PASSES - 1),
                     )
 
+        def look_up(r, tag):
+            old[r] = keep.tile([P, width[r]], F32, name="old_%d" % r, tag=tag, align_bytes=64)
+            nc.vector.tensor_copy(old[r][:], store[:].indirect(entries(slot_sb, *RUNS[r])))
+
         def larger(r, tag):
             new[r] = keep.tile([P, width[r]], F32, name="new_%d" % r, tag=tag, align_bytes=64)
-            nc.vector.tensor_tensor(out=new[r][:], in0=acc[r][:], in1=old[:, RUNS[r][0] : RUNS[r][1]], op=mybir.AluOpType.max)
+            nc.vector.tensor_tensor(out=new[r][:], in0=acc[r][:], in1=old[r][:], op=mybir.AluOpType.max)
 
         def put(r):
             nc.vector.tensor_copy(store[:].indirect(entries(slot_sb, *RUNS[r])), new[r][:])
@@ -166,6 +169,8 @@ def tile_picked_idxput_max_e_kernel(tc, xT, mem, w1_words, w1_scales, offs, slot
         gather_on_vector(0)
         for r in (1, 2):
             gather_on_scalar(0, r)
+        look_up(0, "old_0")
+        look_up(2, "old_2")
         round_plane(1)
         gather_on_vector(1)
         for r in (1, 2):
@@ -173,7 +178,7 @@ def tile_picked_idxput_max_e_kernel(tc, xT, mem, w1_words, w1_scales, offs, slot
         weave(2)
         quantise1(0, "codes1")
         multiply(0)
-        nc.vector.tensor_copy(old[:], store[:].indirect(slot_sb[:]))
+        look_up(1, "plane_1")
         larger(0, "new_0")
         quantise1(1, "codes1")
         multiply(1)

@@ -14,18 +14,15 @@ U8 = mybir.dt.uint8
 FP8X4 = mybir.dt.float8_e4m3fn_x4
 FP4X4 = mybir.dt.float4_e2m1fn_x4
 COPY = mybir.ActivationFunctionType.Copy
+MAX = mybir.AluOpType.max
 
 P = 128
 PASSES = 2
-
-LOADS = [
-    [(0, 1024, 1024), (1024, 2048, 1344)],
-    [(0, 512, 512), (512, 1024, 1024), (1024, 1536, 1536), (1536, 2048, 1696)],
-    [(0, 512, 512), (512, 1024, 1024), (1024, 1536, 1536), (1536, 2048, 2048)],
-]
-PLANE_LOADS = [[(0, 1024), (1024, 2048)], [(0, 1024), (1024, 2048)]]
-WOVEN = (2,)
-RUNS = [(0, 256), (256, 512), (512, 1024)]
+RUN = 256
+RUNS = S // RUN
+REST = S - RUN
+CHUNK = 512
+SPLIT = 576
 
 
 def tile_picked_idxput_max_e_kernel(tc, xT, mem, w1_words, w1_scales, offs, slot, out):
@@ -34,159 +31,105 @@ def tile_picked_idxput_max_e_kernel(tc, xT, mem, w1_words, w1_scales, offs, slot
         keep = ctx.enter_context(tc.tile_pool(name="keep", bufs=1))
         psum = ctx.enter_context(tc.psum_pool(name="psum", bufs=1))
 
-        store = keep.tile([P, U], F32, name="store")
         slot_sb = keep.tile([P, S // 16], U16, name="slot_sb")
         offs_sb = keep.tile([P, S // 16], U16, name="offs_sb")
         w_words = keep.tile([P, PASSES, 2 * N], U8, name="w_words", align_bytes=64)
         w_scales = keep.tile([P, PASSES, N], U8, name="w_scales", align_bytes=64)
+        store_s = keep.tile([P, U], F32, name="store_s", align_bytes=64)
+        store_v = keep.tile([P, U], F32, name="store_v", align_bytes=64)
 
-        x_rows = xT.rearrange("(g p u e) t -> g u p e t", g=PASSES, p=P, u=2, e=2)
-        raw = {}
-        plane = [keep.tile([P, T], F32, name="plane_%d" % e, tag="plane_%d" % e, align_bytes=64) for e in range(2)]
+        x_rows = xT.rearrange("(g p t) c -> g t p c", g=PASSES, p=P, t=4)
+        plane = [keep.tile([P, T], F32, name="plane_%d" % j, align_bytes=64) for j in range(8)]
 
-        def load(pair, c):
-            c0, c1, split = LOADS[pair][c]
-            raw[pair, c] = keep.tile([P, 2, c1 - c0], F32, name="raw_%d_%d" % (pair, c))
-            nc.sync.dma_start(out=raw[pair, c][:], in_=x_rows[pair // 2, pair % 2][:, :, c0:c1])
-
-        def load_plane(e):
-            for c0, c1 in PLANE_LOADS[e]:
-                nc.sync.dma_start(out=plane[e][:, c0:c1], in_=x_rows[1, 1][:, e, c0:c1])
-
-        load(0, 0)
+        nc.sync.dma_start(out=plane[0][:], in_=x_rows[0, 0])
         nc.sync.dma_start(offs_sb[:], offs)
-        for c in range(1, len(LOADS[0])):
-            load(0, c)
-        for pair in range(1, 3):
-            for c in range(len(LOADS[pair])):
-                load(pair, c)
-        load_plane(0)
-        nc.sync.dma_start(slot_sb[:], slot)
-        nc.sync.dma_start(out=store[:], in_=mem)
-        load_plane(1)
-
-        nc.gpsimd.memset(w_scales[:].rearrange("p g n -> p (g n)"), 0)
+        nc.vector.memset(w_scales[:].rearrange("p g n -> p (g n)").bitcast(I32), 0)
         nc.sync.dma_start(out=w_words[:].bitcast(I32), in_=w1_words.rearrange("g p n -> p g n").bitcast(I32))
         for q in range(4):
             nc.sync.dma_start(
                 out=w_scales[32 * q : 32 * q + 4, :, :].bitcast(I32),
                 in_=w1_scales[:, 4 * q : 4 * q + 4, :].rearrange("g r n -> r g n").bitcast(I32),
             )
-
-        width = [j1 - j0 for j0, j1 in RUNS]
-        pairs = [keep.tile([P, T, 2], BF16, name="pairs_%d" % i) for i in range(3)]
-        rounded = [keep.tile([P, T], BF16, name="rounded_%d" % e) for e in range(2)]
-        picked = {r: keep.tile([P, 2, width[r]], U32, name="picked_%d" % r) for r in WOVEN}
-        woven0 = keep.tile([P, S, 2], U32, name="woven0", align_bytes=64)
-        woven1 = [keep.tile([P, width[r], 2], U32, name="woven1_%d" % r, align_bytes=64) for r in range(len(RUNS))]
-        codes0 = keep.tile([P, S], U32, name="codes0", align_bytes=64)
-        scales0 = keep.tile([P, S], U8, name="scales0", align_bytes=64)
-        acc = [psum.tile([P, width[r]], F32, name="acc_%d" % r) for r in range(len(RUNS))]
-        codes1, scales1, old, new = {}, {}, {}, {}
-
-        def cast(pair):
-            for c, (c0, c1, split) in enumerate(LOADS[pair]):
-                src = raw[pair, c][:].rearrange("p e t -> p t e")
-                if split > c0:
-                    nc.scalar.copy(out=pairs[pair][:, c0:split, :], in_=src[:, : split - c0, :])
-                if split < c1:
-                    nc.vector.tensor_copy(out=pairs[pair][:, split:c1, :], in_=src[:, split - c0 :, :])
+        for j in range(1, 8):
+            nc.sync.dma_start(out=plane[j][:], in_=x_rows[j // 4, j % 4])
+        nc.sync.dma_start(slot_sb[:], slot)
+        nc.sync.dma_start(out=store_s[:], in_=mem)
+        nc.sync.dma_start(out=store_v[:], in_=mem)
 
         def entries(lst, j0, j1):
             return lst[:, j0 // 16 : j1 // 16]
 
-        def gather(pair, j0, j1, dst):
-            window = pairs[pair][:].rearrange("p t e -> p (t e)").bitcast(U32)
-            nc.vector.tensor_copy(dst, window.indirect(entries(offs_sb, j0, j1)))
+        woven0 = keep.tile([P, S, 4], BF16, name="woven0", align_bytes=64)
+        woven1 = [keep.tile([P, RUN, 4], BF16, name="woven1_%d" % r, align_bytes=64) for r in range(RUNS)]
+        flat0 = keep.tile([P, 4, REST], BF16, name="flat0", align_bytes=64)
+        flat1 = [keep.tile([P, 2, REST], BF16, name="flat1_%d" % u, align_bytes=64) for u in range(2)]
+        codes0 = keep.tile([P, S], U32, name="codes0", align_bytes=64)
+        scales0 = keep.tile([P, S], U8, name="scales0", align_bytes=64)
+        codes1 = [keep.tile([P, RUN], U32, name="codes1_%d" % r, align_bytes=64) for r in range(RUNS)]
+        scales1 = [keep.tile([P, RUN], U8, name="scales1_%d" % r, align_bytes=64) for r in range(RUNS)]
+        acc = [psum.tile([P, 512], F32, name="acc_%d" % r) for r in range(RUNS)]
+        old = keep.tile([P, S], F32, name="old", align_bytes=64)
+        new = keep.tile([P, S], F32, name="new", align_bytes=64)
 
-        def as_bf16(words):
-            return words.rearrange("p s u -> p (s u)").bitcast(BF16)
+        def gather_vector(j, dst):
+            nc.vector.tensor_copy(dst, plane[j][:].indirect(entries(offs_sb, 0, RUN)))
 
-        def round_plane(e):
-            for c0, c1 in PLANE_LOADS[e]:
-                nc.scalar.copy(out=rounded[e][:, c0:c1], in_=plane[e][:, c0:c1])
+        def gather_scalar(j, dst, j0, j1):
+            nc.scalar.activation(dst, plane[j][:].indirect(entries(offs_sb, j0, j1)), COPY)
 
-        def gather_on_vector(e):
-            four = as_bf16(woven1[0][:]).rearrange("p (s t) -> p s t", t=4)
-            nc.vector.tensor_copy(four[:, :, 2 + e], plane[e][:].indirect(entries(offs_sb, *RUNS[0])))
+        def multiply(g, r, words, scale_bytes):
+            nc.tensor.matmul_mx(
+                out=acc[r][:, :RUN],
+                lhsT=w_words[:, g, :].bitcast(FP4X4),
+                lhsT_scale=w_scales[:, g, :],
+                rhs=words.bitcast(FP8X4),
+                rhs_scale=scale_bytes,
+                start=(g == 0),
+                stop=(g == PASSES - 1),
+            )
 
-        def gather_on_scalar(e, r):
-            if r in WOVEN:
-                dst = picked[r][:, 1, :].bitcast(BF16).rearrange("p (s e) -> p s e", e=2)[:, :, e]
-            else:
-                dst = as_bf16(woven1[r][:]).rearrange("p (s t) -> p s t", t=4)[:, :, 2 + e]
-            nc.scalar.activation(dst, rounded[e][:].indirect(entries(offs_sb, *RUNS[r])), COPY)
+        def weave_pair(u, r):
+            cols = slice((r - 1) * RUN, r * RUN)
+            nc.vector.tensor_copy(out=woven1[r][:, :, 2 * u : 2 * u + 2], in_=flat1[u][:, :, cols].rearrange("p e s -> p s e"))
 
-        def weave(r):
-            nc.scalar.copy(out=woven1[r][:], in_=picked[r][:].rearrange("p u s -> p s u"))
+        def quantise1(r):
+            nc.vector.quantize_mx(out=codes1[r][:].bitcast(FP8X4), scales=scales1[r][:], in_=woven1[r][:].rearrange("p s t -> p (s t)"))
+            multiply(1, r, codes1[r][:], scales1[r][:])
 
-        def quantise0(j0, j1):
-            nc.vector.quantize_mx(out=codes0[:, j0:j1].bitcast(FP8X4), scales=scales0[:, j0:j1], in_=as_bf16(woven0[:, j0:j1, :]))
+        for t in range(4):
+            gather_vector(t, woven0[:, :RUN, t])
+            gather_scalar(t, flat0[:, t, :], RUN, S)
+        gather_vector(4, woven1[0][:, :, 0])
+        gather_scalar(4, flat1[0][:, 0, :], RUN, S)
+        nc.vector.tensor_copy(out=woven0[:, RUN:, :], in_=flat0[:].rearrange("p t s -> p s t"))
+        gather_vector(5, woven1[0][:, :, 1])
+        gather_scalar(5, flat1[0][:, 1, :], RUN, S)
+        nc.vector.quantize_mx(out=codes0[:].bitcast(FP8X4), scales=scales0[:], in_=woven0[:].rearrange("p s t -> p (s t)"))
+        for r in range(RUNS):
+            multiply(0, r, codes0[:, r * RUN : (r + 1) * RUN], scales0[:, r * RUN : (r + 1) * RUN])
+        gather_vector(6, woven1[0][:, :, 2])
+        gather_scalar(6, flat1[1][:, 0, :], RUN, S)
+        for r in range(1, RUNS):
+            weave_pair(0, r)
+        gather_vector(7, woven1[0][:, :, 3])
+        for r in range(1, RUNS):
+            gather_scalar(7, flat1[1][:, 1, (r - 1) * RUN : r * RUN], r * RUN, (r + 1) * RUN)
+        for r in range(1, RUNS):
+            weave_pair(1, r)
+            quantise1(r - 1)
+        quantise1(RUNS - 1)
 
-        def quantise1(r, tag):
-            codes1[r] = keep.tile([P, width[r]], U32, name="codes1_%d" % r, tag=tag, align_bytes=64)
-            scales1[r] = keep.tile([P, width[r]], U8, name="scales1_%d" % r, align_bytes=64)
-            nc.vector.quantize_mx(out=codes1[r][:].bitcast(FP8X4), scales=scales1[r][:], in_=as_bf16(woven1[r][:]))
+        for j0, j1 in ((0, RUN), (RUN, REST)):
+            nc.scalar.activation(old[:, j0:j1], store_s[:].indirect(entries(slot_sb, j0, j1)), COPY)
+        nc.vector.tensor_copy(old[:, REST:], store_s[:].indirect(entries(slot_sb, REST, S)))
+        for r in range(RUNS):
+            cols = slice(r * RUN, (r + 1) * RUN)
+            nc.vector.tensor_tensor(out=new[:, cols], in0=acc[r][:, :RUN], in1=old[:, cols], op=MAX)
+        for j0, j1 in ((0, RUN), (RUN, SPLIT)):
+            nc.scalar.activation(store_s[:].indirect(entries(slot_sb, j0, j1)), new[:, j0:j1], COPY)
+        nc.vector.tensor_copy(store_v[:].indirect(entries(slot_sb, SPLIT, S)), new[:, SPLIT:])
 
-        def multiply(r):
-            n = 512 if width[r] == 512 else 128
-            for c0 in range(0, width[r], n):
-                first = slice(RUNS[r][0] + c0, RUNS[r][0] + c0 + n)
-                second = slice(c0, c0 + n)
-                for g, (words, plane_of_scales) in enumerate(((codes0[:, first], scales0[:, first]), (codes1[r][:, second], scales1[r][:, second]))):
-                    nc.tensor.matmul_mx(
-                        out=acc[r][:, second],
-                        lhsT=w_words[:, g, :].bitcast(FP4X4),
-                        lhsT_scale=w_scales[:, g, :],
-                        rhs=words.bitcast(FP8X4),
-                        rhs_scale=plane_of_scales,
-                        start=(g == 0),
-                        stop=(g == PASSES - 1),
-                    )
-
-        def look_up(r, tag):
-            old[r] = keep.tile([P, width[r]], F32, name="old_%d" % r, tag=tag, align_bytes=64)
-            nc.vector.tensor_copy(old[r][:], store[:].indirect(entries(slot_sb, *RUNS[r])))
-
-        def larger(r, tag):
-            new[r] = keep.tile([P, width[r]], F32, name="new_%d" % r, tag=tag, align_bytes=64)
-            nc.vector.tensor_tensor(out=new[r][:], in0=acc[r][:], in1=old[r][:], op=mybir.AluOpType.max)
-
-        def put(r):
-            nc.vector.tensor_copy(store[:].indirect(entries(slot_sb, *RUNS[r])), new[r][:])
-
-        cast(0)
-        gather(0, 0, S, woven0[:, :, 0])
-        cast(1)
-        for j0 in (0, 512):
-            gather(1, j0, j0 + 512, woven0[:, j0 : j0 + 512, 1])
-        for j0 in (0, 512):
-            quantise0(j0, j0 + 512)
-        cast(2)
-        for r in range(len(RUNS)):
-            gather(2, *RUNS[r], picked[r][:, 0, :] if r in WOVEN else woven1[r][:, :, 0])
-        round_plane(0)
-        gather_on_vector(0)
-        for r in (1, 2):
-            gather_on_scalar(0, r)
-        look_up(0, "old_0")
-        look_up(2, "old_2")
-        round_plane(1)
-        gather_on_vector(1)
-        for r in (1, 2):
-            gather_on_scalar(1, r)
-        weave(2)
-        quantise1(0, "codes1")
-        multiply(0)
-        look_up(1, "plane_1")
-        larger(0, "new_0")
-        quantise1(1, "codes1")
-        multiply(1)
-        put(0)
-        larger(1, "new_1")
-        quantise1(2, "codes1")
-        multiply(2)
-        put(1)
-        larger(2, "new_2")
-        put(2)
-        nc.sync.dma_start(out=out, in_=store[:])
+        for c0 in range(0, U, CHUNK):
+            merged = keep.tile([P, CHUNK], F32, name="merged_%d" % c0, align_bytes=64)
+            nc.vector.tensor_tensor(out=merged[:], in0=store_s[:, c0 : c0 + CHUNK], in1=store_v[:, c0 : c0 + CHUNK], op=MAX)
+            nc.sync.dma_start(out=out[:, c0 : c0 + CHUNK], in_=merged[:])

@@ -20,9 +20,10 @@ P = 128
 PASSES = 2
 RUN = 256
 RUNS = S // RUN
-REST = S - RUN
 CHUNK = 512
-SPLIT = 576
+SPLIT = 736
+EARLY = 384
+FIRST = 768
 
 
 def tile_picked_idxput_max_e_kernel(tc, xT, mem, w1_words, w1_scales, offs, slot, out):
@@ -41,8 +42,8 @@ def tile_picked_idxput_max_e_kernel(tc, xT, mem, w1_words, w1_scales, offs, slot
         x_rows = xT.rearrange("(g p t) c -> g t p c", g=PASSES, p=P, t=4)
         plane = [keep.tile([P, T], F32, name="plane_%d" % j, align_bytes=64) for j in range(8)]
 
-        nc.sync.dma_start(out=plane[0][:], in_=x_rows[0, 0])
         nc.sync.dma_start(offs_sb[:], offs)
+        nc.sync.dma_start(out=plane[0][:], in_=x_rows[0, 0])
         nc.vector.memset(w_scales[:].rearrange("p g n -> p (g n)").bitcast(I32), 0)
         nc.sync.dma_start(out=w_words[:].bitcast(I32), in_=w1_words.rearrange("g p n -> p g n").bitcast(I32))
         for q in range(4):
@@ -53,81 +54,79 @@ def tile_picked_idxput_max_e_kernel(tc, xT, mem, w1_words, w1_scales, offs, slot
         for j in range(1, 8):
             nc.sync.dma_start(out=plane[j][:], in_=x_rows[j // 4, j % 4])
         nc.sync.dma_start(slot_sb[:], slot)
-        nc.sync.dma_start(out=store_s[:], in_=mem)
         nc.sync.dma_start(out=store_v[:], in_=mem)
+        nc.sync.dma_start(out=store_s[:], in_=mem)
 
         def entries(lst, j0, j1):
             return lst[:, j0 // 16 : j1 // 16]
 
-        woven0 = keep.tile([P, S, 4], BF16, name="woven0", align_bytes=64)
-        woven1 = [keep.tile([P, RUN, 4], BF16, name="woven1_%d" % r, align_bytes=64) for r in range(RUNS)]
-        flat0 = keep.tile([P, 4, REST], BF16, name="flat0", align_bytes=64)
-        flat1 = [keep.tile([P, 2, REST], BF16, name="flat1_%d" % u, align_bytes=64) for u in range(2)]
-        codes0 = keep.tile([P, S], U32, name="codes0", align_bytes=64)
-        scales0 = keep.tile([P, S], U8, name="scales0", align_bytes=64)
-        codes1 = [keep.tile([P, RUN], U32, name="codes1_%d" % r, align_bytes=64) for r in range(RUNS)]
-        scales1 = [keep.tile([P, RUN], U8, name="scales1_%d" % r, align_bytes=64) for r in range(RUNS)]
+        woven = [keep.tile([P, S, 4], BF16, name="woven_%d" % g, align_bytes=64) for g in range(PASSES)]
+        flat0 = keep.tile([P, 4, S - EARLY], BF16, name="flat0", align_bytes=64)
+        flat1 = keep.tile([P, 2, S - EARLY], BF16, name="flat1", align_bytes=64)
+        flat2 = keep.tile([P, 2, S - RUN], BF16, name="flat2", align_bytes=64)
+        codes = [keep.tile([P, S], U32, name="codes_%d" % g, align_bytes=64) for g in range(PASSES)]
+        scales = [keep.tile([P, S], U8, name="scales_%d" % g, align_bytes=64) for g in range(PASSES)]
         acc = [psum.tile([P, 512], F32, name="acc_%d" % r) for r in range(RUNS)]
         old = keep.tile([P, S], F32, name="old", align_bytes=64)
         new = keep.tile([P, S], F32, name="new", align_bytes=64)
 
-        def gather_vector(j, dst):
-            nc.vector.tensor_copy(dst, plane[j][:].indirect(entries(offs_sb, 0, RUN)))
+        def gather_vector(j, dst, j0, j1):
+            nc.vector.tensor_copy(dst, plane[j][:].indirect(entries(offs_sb, j0, j1)))
 
         def gather_scalar(j, dst, j0, j1):
             nc.scalar.activation(dst, plane[j][:].indirect(entries(offs_sb, j0, j1)), COPY)
 
-        def multiply(g, r, words, scale_bytes):
-            nc.tensor.matmul_mx(
-                out=acc[r][:, :RUN],
-                lhsT=w_words[:, g, :].bitcast(FP4X4),
-                lhsT_scale=w_scales[:, g, :],
-                rhs=words.bitcast(FP8X4),
-                rhs_scale=scale_bytes,
-                start=(g == 0),
-                stop=(g == PASSES - 1),
+        def weave(dst, rows):
+            nc.vector.tensor_copy(out=dst, in_=rows.rearrange("p t s -> p s t"))
+
+        def quantise(g, j0, j1):
+            nc.vector.quantize_mx(
+                out=codes[g][:, j0:j1].bitcast(FP8X4), scales=scales[g][:, j0:j1], in_=woven[g][:, j0:j1, :].rearrange("p s t -> p (s t)")
             )
+            for r in range(j0 // RUN, j1 // RUN):
+                cols = slice(r * RUN, (r + 1) * RUN)
+                nc.tensor.matmul_mx(
+                    out=acc[r][:, :RUN],
+                    lhsT=w_words[:, g, :].bitcast(FP4X4),
+                    lhsT_scale=w_scales[:, g, :],
+                    rhs=codes[g][:, cols].bitcast(FP8X4),
+                    rhs_scale=scales[g][:, cols],
+                    start=(g == 0),
+                    stop=(g == PASSES - 1),
+                )
 
-        def weave_pair(u, r):
-            cols = slice((r - 1) * RUN, r * RUN)
-            nc.vector.tensor_copy(out=woven1[r][:, :, 2 * u : 2 * u + 2], in_=flat1[u][:, :, cols].rearrange("p e s -> p s e"))
+        gather_vector(0, woven[0][:, :EARLY, 0], 0, EARLY)
+        gather_vector(0, flat0[:, 0, : FIRST - EARLY], EARLY, FIRST)
+        gather_scalar(0, flat0[:, 0, FIRST - EARLY :], FIRST, S)
+        for t in range(1, 4):
+            gather_vector(t, woven[0][:, :EARLY, t], 0, EARLY)
+            gather_scalar(t, flat0[:, t, :], EARLY, S)
+        gather_vector(4, woven[1][:, :EARLY, 0], 0, EARLY)
+        gather_scalar(4, flat1[:, 0, :], EARLY, S)
+        weave(woven[0][:, EARLY:, :], flat0[:])
+        gather_vector(5, woven[1][:, :EARLY, 1], 0, EARLY)
+        gather_scalar(5, flat1[:, 1, :], EARLY, S)
+        quantise(0, 0, S)
+        gather_vector(6, woven[1][:, :RUN, 2], 0, RUN)
+        gather_scalar(6, flat2[:, 0, :], RUN, S)
+        weave(woven[1][:, EARLY:, 0:2], flat1[:])
+        gather_vector(7, woven[1][:, :RUN, 3], 0, RUN)
+        for r in range(1, RUNS):
+            gather_scalar(7, flat2[:, 1, (r - 1) * RUN : r * RUN], r * RUN, (r + 1) * RUN)
+        for r in range(1, RUNS):
+            weave(woven[1][:, r * RUN : (r + 1) * RUN, 2:4], flat2[:, :, (r - 1) * RUN : r * RUN])
+            quantise(1, (r - 1) * RUN, r * RUN)
+        quantise(1, S - RUN, S)
 
-        def quantise1(r):
-            nc.vector.quantize_mx(out=codes1[r][:].bitcast(FP8X4), scales=scales1[r][:], in_=woven1[r][:].rearrange("p s t -> p (s t)"))
-            multiply(1, r, codes1[r][:], scales1[r][:])
-
-        for t in range(4):
-            gather_vector(t, woven0[:, :RUN, t])
-            gather_scalar(t, flat0[:, t, :], RUN, S)
-        gather_vector(4, woven1[0][:, :, 0])
-        gather_scalar(4, flat1[0][:, 0, :], RUN, S)
-        nc.vector.tensor_copy(out=woven0[:, RUN:, :], in_=flat0[:].rearrange("p t s -> p s t"))
-        gather_vector(5, woven1[0][:, :, 1])
-        gather_scalar(5, flat1[0][:, 1, :], RUN, S)
-        nc.vector.quantize_mx(out=codes0[:].bitcast(FP8X4), scales=scales0[:], in_=woven0[:].rearrange("p s t -> p (s t)"))
         for r in range(RUNS):
-            multiply(0, r, codes0[:, r * RUN : (r + 1) * RUN], scales0[:, r * RUN : (r + 1) * RUN])
-        gather_vector(6, woven1[0][:, :, 2])
-        gather_scalar(6, flat1[1][:, 0, :], RUN, S)
-        for r in range(1, RUNS):
-            weave_pair(0, r)
-        gather_vector(7, woven1[0][:, :, 3])
-        for r in range(1, RUNS):
-            gather_scalar(7, flat1[1][:, 1, (r - 1) * RUN : r * RUN], r * RUN, (r + 1) * RUN)
-        for r in range(1, RUNS):
-            weave_pair(1, r)
-            quantise1(r - 1)
-        quantise1(RUNS - 1)
-
-        for j0, j1 in ((0, RUN), (RUN, REST)):
-            nc.scalar.activation(old[:, j0:j1], store_s[:].indirect(entries(slot_sb, j0, j1)), COPY)
-        nc.vector.tensor_copy(old[:, REST:], store_s[:].indirect(entries(slot_sb, REST, S)))
+            cols = slice(r * RUN, (r + 1) * RUN)
+            nc.scalar.activation(old[:, cols], store_v[:].indirect(entries(slot_sb, r * RUN, (r + 1) * RUN)), COPY)
         for r in range(RUNS):
             cols = slice(r * RUN, (r + 1) * RUN)
             nc.vector.tensor_tensor(out=new[:, cols], in0=acc[r][:, :RUN], in1=old[:, cols], op=MAX)
-        for j0, j1 in ((0, RUN), (RUN, SPLIT)):
+        for j0, j1 in ((0, RUN), (SPLIT, S)):
             nc.scalar.activation(store_s[:].indirect(entries(slot_sb, j0, j1)), new[:, j0:j1], COPY)
-        nc.vector.tensor_copy(store_v[:].indirect(entries(slot_sb, SPLIT, S)), new[:, SPLIT:])
+        nc.vector.tensor_copy(store_v[:].indirect(entries(slot_sb, RUN, SPLIT)), new[:, RUN:SPLIT])
 
         for c0 in range(0, U, CHUNK):
             merged = keep.tile([P, CHUNK], F32, name="merged_%d" % c0, align_bytes=64)

@@ -20,9 +20,10 @@ P = 128
 PASSES = 2
 RUN = 256
 RUNS = S // RUN
-CHUNK = 512
+CUTS = (0, 256, 576, 928, 1312, 1696, U)
 SPLIT = 736
-EARLY = 384
+EARLY = 576
+MID = 320
 FIRST = 768
 
 
@@ -45,7 +46,6 @@ def tile_picked_idxput_max_e_kernel(tc, xT, mem, w1_words, w1_scales, offs, slot
         nc.sync.dma_start(offs_sb[:], offs)
         nc.sync.dma_start(out=plane[0][:], in_=x_rows[0, 0])
         nc.vector.memset(w_scales[:].rearrange("p g n -> p (g n)").bitcast(I32), 0)
-        nc.sync.dma_start(out=w_words[:].bitcast(I32), in_=w1_words.rearrange("g p n -> p g n").bitcast(I32))
         for q in range(4):
             nc.sync.dma_start(
                 out=w_scales[32 * q : 32 * q + 4, :, :].bitcast(I32),
@@ -53,6 +53,7 @@ def tile_picked_idxput_max_e_kernel(tc, xT, mem, w1_words, w1_scales, offs, slot
             )
         for j in range(1, 8):
             nc.sync.dma_start(out=plane[j][:], in_=x_rows[j // 4, j % 4])
+        nc.sync.dma_start(out=w_words[:].bitcast(I32), in_=w1_words.rearrange("g p n -> p g n").bitcast(I32))
         nc.sync.dma_start(slot_sb[:], slot)
         nc.sync.dma_start(out=store_v[:], in_=mem)
         nc.sync.dma_start(out=store_s[:], in_=mem)
@@ -62,7 +63,7 @@ def tile_picked_idxput_max_e_kernel(tc, xT, mem, w1_words, w1_scales, offs, slot
 
         woven = [keep.tile([P, S, 4], BF16, name="woven_%d" % g, align_bytes=64) for g in range(PASSES)]
         flat0 = keep.tile([P, 4, S - EARLY], BF16, name="flat0", align_bytes=64)
-        flat1 = keep.tile([P, 2, S - EARLY], BF16, name="flat1", align_bytes=64)
+        flat1 = keep.tile([P, 2, S - MID], BF16, name="flat1", align_bytes=64)
         flat2 = keep.tile([P, 2, S - RUN], BF16, name="flat2", align_bytes=64)
         codes = [keep.tile([P, S], U32, name="codes_%d" % g, align_bytes=64) for g in range(PASSES)]
         scales = [keep.tile([P, S], U8, name="scales_%d" % g, align_bytes=64) for g in range(PASSES)]
@@ -101,15 +102,15 @@ def tile_picked_idxput_max_e_kernel(tc, xT, mem, w1_words, w1_scales, offs, slot
         for t in range(1, 4):
             gather_vector(t, woven[0][:, :EARLY, t], 0, EARLY)
             gather_scalar(t, flat0[:, t, :], EARLY, S)
-        gather_vector(4, woven[1][:, :EARLY, 0], 0, EARLY)
-        gather_scalar(4, flat1[:, 0, :], EARLY, S)
+        gather_vector(4, woven[1][:, :MID, 0], 0, MID)
+        gather_scalar(4, flat1[:, 0, :], MID, S)
         weave(woven[0][:, EARLY:, :], flat0[:])
-        gather_vector(5, woven[1][:, :EARLY, 1], 0, EARLY)
-        gather_scalar(5, flat1[:, 1, :], EARLY, S)
+        gather_vector(5, woven[1][:, :MID, 1], 0, MID)
+        gather_scalar(5, flat1[:, 1, :], MID, S)
         quantise(0, 0, S)
         gather_vector(6, woven[1][:, :RUN, 2], 0, RUN)
         gather_scalar(6, flat2[:, 0, :], RUN, S)
-        weave(woven[1][:, EARLY:, 0:2], flat1[:])
+        weave(woven[1][:, MID:, 0:2], flat1[:])
         gather_vector(7, woven[1][:, :RUN, 3], 0, RUN)
         for r in range(1, RUNS):
             gather_scalar(7, flat2[:, 1, (r - 1) * RUN : r * RUN], r * RUN, (r + 1) * RUN)
@@ -128,7 +129,7 @@ def tile_picked_idxput_max_e_kernel(tc, xT, mem, w1_words, w1_scales, offs, slot
             nc.scalar.activation(store_s[:].indirect(entries(slot_sb, j0, j1)), new[:, j0:j1], COPY)
         nc.vector.tensor_copy(store_v[:].indirect(entries(slot_sb, RUN, SPLIT)), new[:, RUN:SPLIT])
 
-        for c0 in range(0, U, CHUNK):
-            merged = keep.tile([P, CHUNK], F32, name="merged_%d" % c0, align_bytes=64)
-            nc.vector.tensor_tensor(out=merged[:], in0=store_s[:, c0 : c0 + CHUNK], in1=store_v[:, c0 : c0 + CHUNK], op=MAX)
-            nc.sync.dma_start(out=out[:, c0 : c0 + CHUNK], in_=merged[:])
+        for c0, c1 in zip(CUTS, CUTS[1:]):
+            merged = keep.tile([P, c1 - c0], F32, name="merged_%d" % c0, align_bytes=64)
+            nc.vector.tensor_tensor(out=merged[:], in0=store_s[:, c0:c1], in1=store_v[:, c0:c1], op=MAX)
+            nc.sync.dma_start(out=out[:, c0:c1], in_=merged[:])

@@ -21,7 +21,8 @@ PASSES = 2
 RUN = 256
 RUNS = S // RUN
 CUTS = (0, 256, 576, 928, 1312, 1696, U)
-SPLIT = 736
+SPLIT = 768
+LOOK = 896
 EARLY = 576
 MID = 320
 FIRST = 768
@@ -119,9 +120,9 @@ def tile_picked_idxput_max_e_kernel(tc, xT, mem, w1_words, w1_scales, offs, slot
             quantise(1, (r - 1) * RUN, r * RUN)
         quantise(1, S - RUN, S)
 
-        for r in range(RUNS):
-            cols = slice(r * RUN, (r + 1) * RUN)
-            nc.scalar.activation(old[:, cols], store_v[:].indirect(entries(slot_sb, r * RUN, (r + 1) * RUN)), COPY)
+        nc.vector.tensor_copy(old[:, LOOK:], store_v[:].indirect(entries(slot_sb, LOOK, S)))
+        for j0, j1 in ((0, RUN), (RUN, 2 * RUN), (2 * RUN, 3 * RUN), (3 * RUN, LOOK)):
+            nc.scalar.activation(old[:, j0:j1], store_v[:].indirect(entries(slot_sb, j0, j1)), COPY)
         for r in range(RUNS):
             cols = slice(r * RUN, (r + 1) * RUN)
             nc.vector.tensor_tensor(out=new[:, cols], in0=acc[r][:, :RUN], in1=old[:, cols], op=MAX)

@@ -21,8 +21,8 @@ PASSES = 2
 RUN = 256
 RUNS = S // RUN
 CUTS = (0, 256, 576, 928, 1312, 1696, U)
-SPLIT = 768
-LOOK = 896
+SPLIT = 736
+LOOK = (640, 896)
 EARLY = 576
 MID = 320
 FIRST = 768
@@ -120,8 +120,8 @@ def tile_picked_idxput_max_e_kernel(tc, xT, mem, w1_words, w1_scales, offs, slot
             quantise(1, (r - 1) * RUN, r * RUN)
         quantise(1, S - RUN, S)
 
-        nc.vector.tensor_copy(old[:, LOOK:], store_v[:].indirect(entries(slot_sb, LOOK, S)))
-        for j0, j1 in ((0, RUN), (RUN, 2 * RUN), (2 * RUN, 3 * RUN), (3 * RUN, LOOK)):
+        nc.vector.tensor_copy(old[:, LOOK[0] : LOOK[1]], store_v[:].indirect(entries(slot_sb, *LOOK)))
+        for j0, j1 in ((0, RUN), (RUN, 2 * RUN), (2 * RUN, LOOK[0]), (LOOK[1], S)):
             nc.scalar.activation(old[:, j0:j1], store_v[:].indirect(entries(slot_sb, j0, j1)), COPY)
         for r in range(RUNS):
             cols = slice(r * RUN, (r + 1) * RUN)

@@ -20,12 +20,11 @@ P = 128
 PASSES = 2
 RUN = 256
 RUNS = S // RUN
+DIRECT = 384
 CUTS = (0, 256, 576, 928, 1312, 1696, U)
 SPLIT = 736
 LOOK = (640, 896)
-EARLY = 576
-MID = 320
-FIRST = 768
+LOWEST = -(2.0**128 - 2.0**104)
 
 
 def tile_picked_idxput_max_e_kernel(tc, xT, mem, w1_words, w1_scales, offs, slot, out):
@@ -38,34 +37,36 @@ def tile_picked_idxput_max_e_kernel(tc, xT, mem, w1_words, w1_scales, offs, slot
         offs_sb = keep.tile([P, S // 16], U16, name="offs_sb")
         w_words = keep.tile([P, PASSES, 2 * N], U8, name="w_words", align_bytes=64)
         w_scales = keep.tile([P, PASSES, N], U8, name="w_scales", align_bytes=64)
-        store_s = keep.tile([P, U], F32, name="store_s", align_bytes=64)
-        store_v = keep.tile([P, U], F32, name="store_v", align_bytes=64)
+        store = keep.tile([P, U], F32, name="store", align_bytes=64)
+        fresh = keep.tile([P, U], F32, name="fresh", align_bytes=64)
+        lowest = keep.tile([P, 1], F32, name="lowest", align_bytes=64)
 
         x_rows = xT.rearrange("(g p t) c -> g t p c", g=PASSES, p=P, t=4)
         plane = [keep.tile([P, T], F32, name="plane_%d" % j, align_bytes=64) for j in range(8)]
 
-        nc.sync.dma_start(offs_sb[:], offs)
+        scale_rows = keep.tile([4, PASSES * 4, N], U8, name="scale_rows", align_bytes=64)
         nc.sync.dma_start(out=plane[0][:], in_=x_rows[0, 0])
-        nc.vector.memset(w_scales[:].rearrange("p g n -> p (g n)").bitcast(I32), 0)
-        for q in range(4):
-            nc.sync.dma_start(
-                out=w_scales[32 * q : 32 * q + 4, :, :].bitcast(I32),
-                in_=w1_scales[:, 4 * q : 4 * q + 4, :].rearrange("g r n -> r g n").bitcast(I32),
-            )
+        nc.sync.dma_start(offs_sb[:], offs)
+        nc.sync.dma_start(out=scale_rows[:].bitcast(I32), in_=w1_scales.rearrange("g (q r) n -> r (g q) n", r=4).bitcast(I32))
         for j in range(1, 8):
             nc.sync.dma_start(out=plane[j][:], in_=x_rows[j // 4, j % 4])
         nc.sync.dma_start(out=w_words[:].bitcast(I32), in_=w1_words.rearrange("g p n -> p g n").bitcast(I32))
         nc.sync.dma_start(slot_sb[:], slot)
-        nc.sync.dma_start(out=store_v[:], in_=mem)
-        nc.sync.dma_start(out=store_s[:], in_=mem)
+        nc.sync.dma_start(out=store[:], in_=mem)
+
+        nc.vector.memset(w_scales[:].rearrange("p g n -> p (g n)").bitcast(I32), 0)
+        for q in range(4):
+            nc.vector.tensor_copy(out=w_scales[32 * q : 32 * q + 4, :, :].bitcast(I32), in_=scale_rows[:, q::4, :].bitcast(I32))
+
+        nc.vector.memset(lowest[:], LOWEST)
+        nc.scalar.activation(fresh[:], lowest[:].to_broadcast([P, U]), COPY)
 
         def entries(lst, j0, j1):
             return lst[:, j0 // 16 : j1 // 16]
 
         woven = [keep.tile([P, S, 4], BF16, name="woven_%d" % g, align_bytes=64) for g in range(PASSES)]
-        flat0 = keep.tile([P, 4, S - EARLY], BF16, name="flat0", align_bytes=64)
-        flat1 = keep.tile([P, 2, S - MID], BF16, name="flat1", align_bytes=64)
-        flat2 = keep.tile([P, 2, S - RUN], BF16, name="flat2", align_bytes=64)
+        flat = [keep.tile([P, 2, S - DIRECT], BF16, name="flat_%d" % h, align_bytes=64) for h in range(3)]
+        last = keep.tile([P, 2, S - RUN], BF16, name="last", align_bytes=64)
         codes = [keep.tile([P, S], U32, name="codes_%d" % g, align_bytes=64) for g in range(PASSES)]
         scales = [keep.tile([P, S], U8, name="scales_%d" % g, align_bytes=64) for g in range(PASSES)]
         acc = [psum.tile([P, 512], F32, name="acc_%d" % r) for r in range(RUNS)]
@@ -97,40 +98,36 @@ def tile_picked_idxput_max_e_kernel(tc, xT, mem, w1_words, w1_scales, offs, slot
                     stop=(g == PASSES - 1),
                 )
 
-        gather_vector(0, woven[0][:, :EARLY, 0], 0, EARLY)
-        gather_vector(0, flat0[:, 0, : FIRST - EARLY], EARLY, FIRST)
-        gather_scalar(0, flat0[:, 0, FIRST - EARLY :], FIRST, S)
-        for t in range(1, 4):
-            gather_vector(t, woven[0][:, :EARLY, t], 0, EARLY)
-            gather_scalar(t, flat0[:, t, :], EARLY, S)
-        gather_vector(4, woven[1][:, :MID, 0], 0, MID)
-        gather_scalar(4, flat1[:, 0, :], MID, S)
-        weave(woven[0][:, EARLY:, :], flat0[:])
-        gather_vector(5, woven[1][:, :MID, 1], 0, MID)
-        gather_scalar(5, flat1[:, 1, :], MID, S)
-        quantise(0, 0, S)
+        for j in range(6):
+            g, t, h = j // 4, j % 4, j // 2
+            gather_vector(j, woven[g][:, :DIRECT, t], 0, DIRECT)
+            gather_scalar(j, flat[h][:, j % 2, :], DIRECT, S)
+            if j % 2 == 1:
+                weave(woven[g][:, DIRECT:, t - 1 : t + 1], flat[h][:])
+            if j == 4:
+                quantise(0, 0, S)
         gather_vector(6, woven[1][:, :RUN, 2], 0, RUN)
-        gather_scalar(6, flat2[:, 0, :], RUN, S)
-        weave(woven[1][:, MID:, 0:2], flat1[:])
+        gather_vector(6, last[:, 0, : DIRECT - RUN], RUN, DIRECT)
+        gather_scalar(6, last[:, 0, DIRECT - RUN :], DIRECT, S)
         gather_vector(7, woven[1][:, :RUN, 3], 0, RUN)
         for r in range(1, RUNS):
-            gather_scalar(7, flat2[:, 1, (r - 1) * RUN : r * RUN], r * RUN, (r + 1) * RUN)
+            gather_scalar(7, last[:, 1, (r - 1) * RUN : r * RUN], r * RUN, (r + 1) * RUN)
         for r in range(1, RUNS):
-            weave(woven[1][:, r * RUN : (r + 1) * RUN, 2:4], flat2[:, :, (r - 1) * RUN : r * RUN])
+            weave(woven[1][:, r * RUN : (r + 1) * RUN, 2:4], last[:, :, (r - 1) * RUN : r * RUN])
             quantise(1, (r - 1) * RUN, r * RUN)
         quantise(1, S - RUN, S)
 
-        nc.vector.tensor_copy(old[:, LOOK[0] : LOOK[1]], store_v[:].indirect(entries(slot_sb, *LOOK)))
+        nc.vector.tensor_copy(old[:, LOOK[0] : LOOK[1]], store[:].indirect(entries(slot_sb, *LOOK)))
         for j0, j1 in ((0, RUN), (RUN, 2 * RUN), (2 * RUN, LOOK[0]), (LOOK[1], S)):
-            nc.scalar.activation(old[:, j0:j1], store_v[:].indirect(entries(slot_sb, j0, j1)), COPY)
+            nc.scalar.activation(old[:, j0:j1], store[:].indirect(entries(slot_sb, j0, j1)), COPY)
         for r in range(RUNS):
             cols = slice(r * RUN, (r + 1) * RUN)
             nc.vector.tensor_tensor(out=new[:, cols], in0=acc[r][:, :RUN], in1=old[:, cols], op=MAX)
         for j0, j1 in ((0, RUN), (SPLIT, S)):
-            nc.scalar.activation(store_s[:].indirect(entries(slot_sb, j0, j1)), new[:, j0:j1], COPY)
-        nc.vector.tensor_copy(store_v[:].indirect(entries(slot_sb, RUN, SPLIT)), new[:, RUN:SPLIT])
+            nc.scalar.activation(fresh[:].indirect(entries(slot_sb, j0, j1)), new[:, j0:j1], COPY)
+        nc.vector.tensor_copy(store[:].indirect(entries(slot_sb, RUN, SPLIT)), new[:, RUN:SPLIT])
 
         for c0, c1 in zip(CUTS, CUTS[1:]):
             merged = keep.tile([P, c1 - c0], F32, name="merged_%d" % c0, align_bytes=64)
-            nc.vector.tensor_tensor(out=merged[:], in0=store_s[:, c0:c1], in1=store_v[:, c0:c1], op=MAX)
+            nc.vector.tensor_tensor(out=merged[:], in0=fresh[:, c0:c1], in1=store[:, c0:c1], op=MAX)
             nc.sync.dma_start(out=out[:, c0:c1], in_=merged[:])

@@ -35,16 +35,16 @@ def tile_picked_idxput_max_e_kernel(tc, xT, mem, w1_words, w1_scales, offs, slot
 
         slot_sb = keep.tile([P, S // 16], U16, name="slot_sb")
         offs_sb = keep.tile([P, S // 16], U16, name="offs_sb")
-        w_words = keep.tile([P, PASSES, 2 * N], U8, name="w_words", align_bytes=64)
-        w_scales = keep.tile([P, PASSES, N], U8, name="w_scales", align_bytes=64)
-        store = keep.tile([P, U], F32, name="store", align_bytes=64)
-        fresh = keep.tile([P, U], F32, name="fresh", align_bytes=64)
-        lowest = keep.tile([P, 1], F32, name="lowest", align_bytes=64)
+        w_words = keep.tile([P, PASSES, 2 * N], U8, name="w_words", align_bytes=256)
+        w_scales = keep.tile([P, PASSES, N], U8, name="w_scales", align_bytes=256)
+        store = keep.tile([P, U], F32, name="store", align_bytes=256)
+        fresh = keep.tile([P, U], F32, name="fresh", align_bytes=256)
+        lowest = keep.tile([P, 1], F32, name="lowest", align_bytes=256)
 
         x_rows = xT.rearrange("(g p t) c -> g t p c", g=PASSES, p=P, t=4)
-        plane = [keep.tile([P, T], F32, name="plane_%d" % j, align_bytes=64) for j in range(8)]
+        plane = [keep.tile([P, T], F32, name="plane_%d" % j, align_bytes=256) for j in range(8)]
 
-        scale_rows = keep.tile([4, PASSES * 4, N], U8, name="scale_rows", align_bytes=64)
+        scale_rows = keep.tile([4, PASSES * 4, N], U8, name="scale_rows", align_bytes=256)
         nc.sync.dma_start(out=plane[0][:], in_=x_rows[0, 0])
         nc.sync.dma_start(offs_sb[:], offs)
         nc.sync.dma_start(out=scale_rows[:].bitcast(I32), in_=w1_scales.rearrange("g (q r) n -> r (g q) n", r=4).bitcast(I32))
@@ -64,14 +64,14 @@ def tile_picked_idxput_max_e_kernel(tc, xT, mem, w1_words, w1_scales, offs, slot
         def entries(lst, j0, j1):
             return lst[:, j0 // 16 : j1 // 16]
 
-        woven = [keep.tile([P, S, 4], BF16, name="woven_%d" % g, align_bytes=64) for g in range(PASSES)]
-        flat = [keep.tile([P, 2, S - DIRECT], BF16, name="flat_%d" % h, align_bytes=64) for h in range(3)]
-        last = keep.tile([P, 2, S - RUN], BF16, name="last", align_bytes=64)
-        codes = [keep.tile([P, S], U32, name="codes_%d" % g, align_bytes=64) for g in range(PASSES)]
-        scales = [keep.tile([P, S], U8, name="scales_%d" % g, align_bytes=64) for g in range(PASSES)]
+        woven = [keep.tile([P, S, 4], BF16, name="woven_%d" % g, align_bytes=256) for g in range(PASSES)]
+        flat = [keep.tile([P, 2, S - DIRECT], BF16, name="flat_%d" % h, align_bytes=256) for h in range(3)]
+        last = keep.tile([P, 2, S - RUN], BF16, name="last", align_bytes=256)
+        codes = [keep.tile([P, S], U32, name="codes_%d" % g, align_bytes=256) for g in range(PASSES)]
+        scales = [keep.tile([P, S], U8, name="scales_%d" % g, align_bytes=256) for g in range(PASSES)]
         acc = [psum.tile([P, 512], F32, name="acc_%d" % r) for r in range(RUNS)]
-        old = keep.tile([P, S], F32, name="old", align_bytes=64)
-        new = keep.tile([P, S], F32, name="new", align_bytes=64)
+        old = keep.tile([P, S], F32, name="old", align_bytes=256)
+        new = keep.tile([P, S], F32, name="new", align_bytes=256)
 
         def gather_vector(j, dst, j0, j1):
             nc.vector.tensor_copy(dst, plane[j][:].indirect(entries(offs_sb, j0, j1)))
@@ -128,6 +128,6 @@ def tile_picked_idxput_max_e_kernel(tc, xT, mem, w1_words, w1_scales, offs, slot
         nc.vector.tensor_copy(store[:].indirect(entries(slot_sb, RUN, SPLIT)), new[:, RUN:SPLIT])
 
         for c0, c1 in zip(CUTS, CUTS[1:]):
-            merged = keep.tile([P, c1 - c0], F32, name="merged_%d" % c0, align_bytes=64)
+            merged = keep.tile([P, c1 - c0], F32, name="merged_%d" % c0, align_bytes=256)
             nc.vector.tensor_tensor(out=merged[:], in0=fresh[:, c0:c1], in1=store[:, c0:c1], op=MAX)
             nc.sync.dma_start(out=out[:, c0:c1], in_=merged[:])

@@ -20,7 +20,9 @@ P = 128
 PASSES = 2
 RUN = 256
 RUNS = S // RUN
-DIRECT = 384
+DIRECT = (512, 512, 320)
+HALF = 672
+HELP = 384
 CUTS = (0, 256, 576, 928, 1312, 1696, U)
 SPLIT = 736
 LOOK = (640, 896)
@@ -45,9 +47,9 @@ def tile_picked_idxput_max_e_kernel(tc, xT, mem, w1_words, w1_scales, offs, slot
         plane = [keep.tile([P, T], F32, name="plane_%d" % j, align_bytes=256) for j in range(8)]
 
         scale_rows = keep.tile([4, PASSES * 4, N], U8, name="scale_rows", align_bytes=256)
+        nc.sync.dma_start(out=scale_rows[:].bitcast(I32), in_=w1_scales.rearrange("g (q r) n -> r (g q) n", r=4).bitcast(I32))
         nc.sync.dma_start(out=plane[0][:], in_=x_rows[0, 0])
         nc.sync.dma_start(offs_sb[:], offs)
-        nc.sync.dma_start(out=scale_rows[:].bitcast(I32), in_=w1_scales.rearrange("g (q r) n -> r (g q) n", r=4).bitcast(I32))
         for j in range(1, 8):
             nc.sync.dma_start(out=plane[j][:], in_=x_rows[j // 4, j % 4])
         nc.sync.dma_start(out=w_words[:].bitcast(I32), in_=w1_words.rearrange("g p n -> p g n").bitcast(I32))
@@ -65,7 +67,7 @@ def tile_picked_idxput_max_e_kernel(tc, xT, mem, w1_words, w1_scales, offs, slot
             return lst[:, j0 // 16 : j1 // 16]
 
         woven = [keep.tile([P, S, 4], BF16, name="woven_%d" % g, align_bytes=256) for g in range(PASSES)]
-        flat = [keep.tile([P, 2, S - DIRECT], BF16, name="flat_%d" % h, align_bytes=256) for h in range(3)]
+        flat = [keep.tile([P, 2, S - DIRECT[h]], BF16, name="flat_%d" % h, align_bytes=256) for h in range(3)]
         last = keep.tile([P, 2, S - RUN], BF16, name="last", align_bytes=256)
         codes = [keep.tile([P, S], U32, name="codes_%d" % g, align_bytes=256) for g in range(PASSES)]
         scales = [keep.tile([P, S], U8, name="scales_%d" % g, align_bytes=256) for g in range(PASSES)]
@@ -98,17 +100,20 @@ def tile_picked_idxput_max_e_kernel(tc, xT, mem, w1_words, w1_scales, offs, slot
                     stop=(g == PASSES - 1),
                 )
 
-        for j in range(6):
+        for j in range(5):
             g, t, h = j // 4, j % 4, j // 2
-            gather_vector(j, woven[g][:, :DIRECT, t], 0, DIRECT)
-            gather_scalar(j, flat[h][:, j % 2, :], DIRECT, S)
+            gather_vector(j, woven[g][:, : DIRECT[h], t], 0, DIRECT[h])
+            gather_scalar(j, flat[h][:, j % 2, :], DIRECT[h], S)
             if j % 2 == 1:
-                weave(woven[g][:, DIRECT:, t - 1 : t + 1], flat[h][:])
-            if j == 4:
-                quantise(0, 0, S)
+                weave(woven[g][:, DIRECT[h] :, t - 1 : t + 1], flat[h][:])
+        quantise(0, 0, S)
+        gather_vector(5, woven[1][:, : DIRECT[2], 1], 0, DIRECT[2])
+        for j0, j1 in ((DIRECT[2], HALF), (HALF, S)):
+            gather_scalar(5, flat[2][:, 1, j0 - DIRECT[2] : j1 - DIRECT[2]], j0, j1)
+            weave(woven[1][:, j0:j1, 0:2], flat[2][:, :, j0 - DIRECT[2] : j1 - DIRECT[2]])
         gather_vector(6, woven[1][:, :RUN, 2], 0, RUN)
-        gather_vector(6, last[:, 0, : DIRECT - RUN], RUN, DIRECT)
-        gather_scalar(6, last[:, 0, DIRECT - RUN :], DIRECT, S)
+        gather_vector(6, last[:, 0, : HELP - RUN], RUN, HELP)
+        gather_scalar(6, last[:, 0, HELP - RUN :], HELP, S)
         gather_vector(7, woven[1][:, :RUN, 3], 0, RUN)
         for r in range(1, RUNS):
             gather_scalar(7, last[:, 1, (r - 1) * RUN : r * RUN], r * RUN, (r + 1) * RUN)

@@ -15,6 +15,8 @@ FP8X4 = mybir.dt.float8_e4m3fn_x4
 FP4X4 = mybir.dt.float4_e2m1fn_x4
 COPY = mybir.ActivationFunctionType.Copy
 MAX = mybir.AluOpType.max
+MULT = mybir.AluOpType.mult
+ADD = mybir.AluOpType.add
 
 P = 128
 PASSES = 2
@@ -22,7 +24,8 @@ RUN = 256
 RUNS = S // RUN
 DIRECT = (512, 512, 320)
 HALF = 672
-HELP = 384
+LEAD = 128
+POOLED = 256
 CUTS = (0, 256, 576, 928, 1312, 1696, U)
 SPLIT = 736
 LOOK = (640, 896)
@@ -100,26 +103,39 @@ def tile_picked_idxput_max_e_kernel(tc, xT, mem, w1_words, w1_scales, offs, slot
                     stop=(g == PASSES - 1),
                 )
 
-        for j in range(5):
-            g, t, h = j // 4, j % 4, j // 2
-            gather_vector(j, woven[g][:, : DIRECT[h], t], 0, DIRECT[h])
-            gather_scalar(j, flat[h][:, j % 2, :], DIRECT[h], S)
+        for j in range(4):
+            gather_vector(j, woven[0][:, : DIRECT[0], j], 0, DIRECT[0])
+            gather_scalar(j, flat[j // 2][:, j % 2, :POOLED], DIRECT[0], DIRECT[0] + POOLED)
+            gather_scalar(j, flat[j // 2][:, j % 2, POOLED:], DIRECT[0] + POOLED, S)
             if j % 2 == 1:
-                weave(woven[g][:, DIRECT[h] :, t - 1 : t + 1], flat[h][:])
+                nc.gpsimd.tensor_scalar(
+                    out=woven[0][:, DIRECT[0] : DIRECT[0] + POOLED, j - 1 : j + 1],
+                    in0=flat[j // 2][:, :, :POOLED].rearrange("p t s -> p s t"),
+                    scalar1=1.0,
+                    scalar2=0.0,
+                    op0=MULT,
+                    op1=ADD,
+                )
+                weave(woven[0][:, DIRECT[0] + POOLED :, j - 1 : j + 1], flat[j // 2][:, :, POOLED:])
+        gather_vector(4, woven[1][:, : DIRECT[2], 0], 0, DIRECT[2])
+        gather_scalar(4, flat[2][:, 0, :], DIRECT[2], S)
         quantise(0, 0, S)
         gather_vector(5, woven[1][:, : DIRECT[2], 1], 0, DIRECT[2])
         for j0, j1 in ((DIRECT[2], HALF), (HALF, S)):
             gather_scalar(5, flat[2][:, 1, j0 - DIRECT[2] : j1 - DIRECT[2]], j0, j1)
             weave(woven[1][:, j0:j1, 0:2], flat[2][:, :, j0 - DIRECT[2] : j1 - DIRECT[2]])
-        gather_vector(6, woven[1][:, :RUN, 2], 0, RUN)
-        gather_vector(6, last[:, 0, : HELP - RUN], RUN, HELP)
-        gather_scalar(6, last[:, 0, HELP - RUN :], HELP, S)
-        gather_vector(7, woven[1][:, :RUN, 3], 0, RUN)
-        for r in range(1, RUNS):
-            gather_scalar(7, last[:, 1, (r - 1) * RUN : r * RUN], r * RUN, (r + 1) * RUN)
-        for r in range(1, RUNS):
-            weave(woven[1][:, r * RUN : (r + 1) * RUN, 2:4], last[:, :, (r - 1) * RUN : r * RUN])
-            quantise(1, (r - 1) * RUN, r * RUN)
+        gather_vector(6, woven[1][:, LEAD : LEAD + RUN, 2], LEAD, LEAD + RUN)
+        gather_vector(6, last[:, 0, :LEAD], 0, LEAD)
+        gather_scalar(6, last[:, 0, LEAD:], LEAD + RUN, S)
+        gather_vector(7, woven[1][:, LEAD : LEAD + RUN, 3], LEAD, LEAD + RUN)
+        pieces = ((0, LEAD), (LEAD + RUN, 2 * RUN), (2 * RUN, 3 * RUN), (3 * RUN, S))
+        rows = [last[:, :, j0 - (RUN if j0 else 0) : j1 - (RUN if j0 else 0)] for j0, j1 in pieces]
+        for (j0, j1), row in zip(pieces, rows):
+            gather_scalar(7, row[:, 1, :], j0, j1)
+        for r, ((j0, j1), row) in enumerate(zip(pieces, rows)):
+            weave(woven[1][:, j0:j1, 2:4], row)
+            if r > 0:
+                quantise(1, (r - 1) * RUN, r * RUN)
         quantise(1, S - RUN, S)
 
         nc.vector.tensor_copy(old[:, LOOK[0] : LOOK[1]], store[:].indirect(entries(slot_sb, *LOOK)))

@@ -26,7 +26,7 @@ DIRECT = (512, 512, 320)
 HALF = 672
 LEAD = 128
 POOLED = 256
-CUTS = (0, 256, 576, 928, 1312, 1696, U)
+CUTS = (0, 240, 560, 928, 1328, 1728, U)
 SPLIT = 736
 LOOK = (640, 896)
 LOWEST = -(2.0**128 - 2.0**104)
@@ -40,7 +40,7 @@ def tile_picked_idxput_max_e_kernel(tc, xT, mem, w1_words, w1_scales, offs, slot
 
         slot_sb = keep.tile([P, S // 16], U16, name="slot_sb")
         offs_sb = keep.tile([P, S // 16], U16, name="offs_sb")
-        w_words = keep.tile([P, PASSES, 2 * N], U8, name="w_words", align_bytes=256)
+        w_words = [keep.tile([P, 2 * N], U8, name="w_words_%d" % g, align_bytes=256) for g in range(PASSES)]
         w_scales = keep.tile([P, PASSES, N], U8, name="w_scales", align_bytes=256)
         store = keep.tile([P, U], F32, name="store", align_bytes=256)
         fresh = keep.tile([P, U], F32, name="fresh", align_bytes=256)
@@ -50,14 +50,15 @@ def tile_picked_idxput_max_e_kernel(tc, xT, mem, w1_words, w1_scales, offs, slot
         plane = [keep.tile([P, T], F32, name="plane_%d" % j, align_bytes=256) for j in range(8)]
 
         scale_rows = keep.tile([4, PASSES * 4, N], U8, name="scale_rows", align_bytes=256)
-        nc.sync.dma_start(out=scale_rows[:].bitcast(I32), in_=w1_scales.rearrange("g (q r) n -> r (g q) n", r=4).bitcast(I32))
+        nc.scalar.dma_start(out=scale_rows[:].bitcast(I32), in_=w1_scales.rearrange("g (q r) n -> r (g q) n", r=4).bitcast(I32))
         nc.sync.dma_start(out=plane[0][:], in_=x_rows[0, 0])
         nc.sync.dma_start(offs_sb[:], offs)
         for j in range(1, 8):
             nc.sync.dma_start(out=plane[j][:], in_=x_rows[j // 4, j % 4])
-        nc.sync.dma_start(out=w_words[:].bitcast(I32), in_=w1_words.rearrange("g p n -> p g n").bitcast(I32))
+        nc.sync.dma_start(out=w_words[0][:].bitcast(I32), in_=w1_words[0].bitcast(I32))
         nc.sync.dma_start(slot_sb[:], slot)
         nc.sync.dma_start(out=store[:], in_=mem)
+        nc.sync.dma_start(out=w_words[1][:].bitcast(I32), in_=w1_words[1].bitcast(I32))
 
         nc.vector.memset(w_scales[:].rearrange("p g n -> p (g n)").bitcast(I32), 0)
         for q in range(4):
@@ -95,7 +96,7 @@ def tile_picked_idxput_max_e_kernel(tc, xT, mem, w1_words, w1_scales, offs, slot
                 cols = slice(r * RUN, (r + 1) * RUN)
                 nc.tensor.matmul_mx(
                     out=acc[r][:, :RUN],
-                    lhsT=w_words[:, g, :].bitcast(FP4X4),
+                    lhsT=w_words[g][:].bitcast(FP4X4),
                     lhsT_scale=w_scales[:, g, :],
                     rhs=codes[g][:, cols].bitcast(FP8X4),
                     rhs_scale=scales[g][:, cols],
@@ -124,18 +125,17 @@ def tile_picked_idxput_max_e_kernel(tc, xT, mem, w1_words, w1_scales, offs, slot
         for j0, j1 in ((DIRECT[2], HALF), (HALF, S)):
             gather_scalar(5, flat[2][:, 1, j0 - DIRECT[2] : j1 - DIRECT[2]], j0, j1)
             weave(woven[1][:, j0:j1, 0:2], flat[2][:, :, j0 - DIRECT[2] : j1 - DIRECT[2]])
-        gather_vector(6, woven[1][:, LEAD : LEAD + RUN, 2], LEAD, LEAD + RUN)
-        gather_vector(6, last[:, 0, :LEAD], 0, LEAD)
+        gather_vector(6, woven[1][:, : LEAD + RUN, 2], 0, LEAD + RUN)
         gather_scalar(6, last[:, 0, LEAD:], LEAD + RUN, S)
         gather_vector(7, woven[1][:, LEAD : LEAD + RUN, 3], LEAD, LEAD + RUN)
-        pieces = ((0, LEAD), (LEAD + RUN, 2 * RUN), (2 * RUN, 3 * RUN), (3 * RUN, S))
-        rows = [last[:, :, j0 - (RUN if j0 else 0) : j1 - (RUN if j0 else 0)] for j0, j1 in pieces]
-        for (j0, j1), row in zip(pieces, rows):
-            gather_scalar(7, row[:, 1, :], j0, j1)
-        for r, ((j0, j1), row) in enumerate(zip(pieces, rows)):
-            weave(woven[1][:, j0:j1, 2:4], row)
-            if r > 0:
-                quantise(1, (r - 1) * RUN, r * RUN)
+        pieces = ((LEAD + RUN, 2 * RUN), (2 * RUN, 3 * RUN), (3 * RUN, S))
+        gather_scalar(7, last[:, 1, :LEAD], 0, LEAD)
+        for j0, j1 in pieces:
+            gather_scalar(7, last[:, 1, j0 - RUN : j1 - RUN], j0, j1)
+        nc.vector.tensor_copy(out=woven[1][:, :LEAD, 3], in_=last[:, 1, :LEAD])
+        for r, (j0, j1) in enumerate(pieces):
+            weave(woven[1][:, j0:j1, 2:4], last[:, :, j0 - RUN : j1 - RUN])
+            quantise(1, r * RUN, (r + 1) * RUN)
         quantise(1, S - RUN, S)
 
         nc.vector.tensor_copy(old[:, LOOK[0] : LOOK[1]], store[:].indirect(entries(slot_sb, *LOOK)))

@@ -28,7 +28,7 @@ LEAD = 128
 POOLED = 256
 CUTS = (0, 240, 560, 928, 1328, 1728, U)
 SPLIT = 736
-LOOK = (640, 896)
+LOOK = (640, 864)
 LOWEST = -(2.0**128 - 2.0**104)
 
 
@@ -51,11 +51,11 @@ def tile_picked_idxput_max_e_kernel(tc, xT, mem, w1_words, w1_scales, offs, slot
 
         scale_rows = keep.tile([4, PASSES * 4, N], U8, name="scale_rows", align_bytes=256)
         nc.scalar.dma_start(out=scale_rows[:].bitcast(I32), in_=w1_scales.rearrange("g (q r) n -> r (g q) n", r=4).bitcast(I32))
+        nc.scalar.dma_start(out=w_words[0][:].bitcast(I32), in_=w1_words[0].bitcast(I32))
         nc.sync.dma_start(out=plane[0][:], in_=x_rows[0, 0])
         nc.sync.dma_start(offs_sb[:], offs)
         for j in range(1, 8):
             nc.sync.dma_start(out=plane[j][:], in_=x_rows[j // 4, j % 4])
-        nc.sync.dma_start(out=w_words[0][:].bitcast(I32), in_=w1_words[0].bitcast(I32))
         nc.sync.dma_start(slot_sb[:], slot)
         nc.sync.dma_start(out=store[:], in_=mem)
         nc.sync.dma_start(out=w_words[1][:].bitcast(I32), in_=w1_words[1].bitcast(I32))

@@ -28,7 +28,7 @@ LEAD = 128
 POOLED = 256
 CUTS = (0, 240, 560, 928, 1328, 1728, U)
 SPLIT = 736
-LOOK = (640, 864)
+LOOK = (672, 832)
 LOWEST = -(2.0**128 - 2.0**104)
 
 

@@ -135,8 +135,9 @@ def tile_picked_idxput_max_e_kernel(tc, xT, mem, w1_words, w1_scales, offs, slot
         nc.vector.tensor_copy(out=woven[1][:, :LEAD, 3], in_=last[:, 1, :LEAD])
         for r, (j0, j1) in enumerate(pieces):
             weave(woven[1][:, j0:j1, 2:4], last[:, :, j0 - RUN : j1 - RUN])
-            quantise(1, r * RUN, (r + 1) * RUN)
-        quantise(1, S - RUN, S)
+            if r != 1:
+                quantise(1, r * RUN, (r + 1) * RUN)
+                quantise(1, (r + 1) * RUN, (r + 2) * RUN)
 
         nc.vector.tensor_copy(old[:, LOOK[0] : LOOK[1]], store[:].indirect(entries(slot_sb, *LOOK)))
         for j0, j1 in ((0, RUN), (RUN, 2 * RUN), (2 * RUN, LOOK[0]), (LOOK[1], S)):

@@ -22,8 +22,8 @@ P = 128
 PASSES = 2
 RUN = 256
 RUNS = S // RUN
-DIRECT = (512, 512, 320)
-HALF = 672
+DIRECT = (512, 512, 256)
+HALF = 640
 LEAD = 128
 POOLED = 256
 CUTS = (0, 240, 560, 928, 1328, 1728, U)
@@ -125,14 +125,15 @@ def tile_picked_idxput_max_e_kernel(tc, xT, mem, w1_words, w1_scales, offs, slot
         for j0, j1 in ((DIRECT[2], HALF), (HALF, S)):
             gather_scalar(5, flat[2][:, 1, j0 - DIRECT[2] : j1 - DIRECT[2]], j0, j1)
             weave(woven[1][:, j0:j1, 0:2], flat[2][:, :, j0 - DIRECT[2] : j1 - DIRECT[2]])
-        gather_vector(6, woven[1][:, : LEAD + RUN, 2], 0, LEAD + RUN)
+        gather_vector(6, woven[1][:, LEAD : LEAD + RUN, 2], LEAD, LEAD + RUN)
+        gather_scalar(6, last[:, 0, :LEAD], 0, LEAD)
         gather_scalar(6, last[:, 0, LEAD:], LEAD + RUN, S)
         gather_vector(7, woven[1][:, LEAD : LEAD + RUN, 3], LEAD, LEAD + RUN)
         pieces = ((LEAD + RUN, 2 * RUN), (2 * RUN, 3 * RUN), (3 * RUN, S))
         gather_scalar(7, last[:, 1, :LEAD], 0, LEAD)
         for j0, j1 in pieces:
             gather_scalar(7, last[:, 1, j0 - RUN : j1 - RUN], j0, j1)
-        nc.vector.tensor_copy(out=woven[1][:, :LEAD, 3], in_=last[:, 1, :LEAD])
+        weave(woven[1][:, :LEAD, 2:4], last[:, :, :LEAD])
         for r, (j0, j1) in enumerate(pieces):
             weave(woven[1][:, j0:j1, 2:4], last[:, :, j0 - RUN : j1 - RUN])
             if r != 1:

@@ -27,8 +27,7 @@ HALF = 640
 LEAD = 128
 POOLED = 256
 CUTS = (0, 240, 560, 928, 1328, 1728, U)
-SPLIT = 736
-LOOK = (672, 832)
+SPLIT = 704
 LOWEST = -(2.0**128 - 2.0**104)
 
 
@@ -73,10 +72,10 @@ def tile_picked_idxput_max_e_kernel(tc, xT, mem, w1_words, w1_scales, offs, slot
         woven = [keep.tile([P, S, 4], BF16, name="woven_%d" % g, align_bytes=256) for g in range(PASSES)]
         flat = [keep.tile([P, 2, S - DIRECT[h]], BF16, name="flat_%d" % h, align_bytes=256) for h in range(3)]
         last = keep.tile([P, 2, S - RUN], BF16, name="last", align_bytes=256)
-        codes = [keep.tile([P, S], U32, name="codes_%d" % g, align_bytes=256) for g in range(PASSES)]
+        codes_first = keep.tile([P, S], U32, name="codes_first", align_bytes=256)
+        codes_second = [keep.tile([P, RUN], U32, name="codes_second_%d" % r, tag="codes_second_%d" % r, align_bytes=256) for r in range(RUNS)]
         scales = [keep.tile([P, S], U8, name="scales_%d" % g, align_bytes=256) for g in range(PASSES)]
         acc = [psum.tile([P, 512], F32, name="acc_%d" % r) for r in range(RUNS)]
-        old = keep.tile([P, S], F32, name="old", align_bytes=256)
         new = keep.tile([P, S], F32, name="new", align_bytes=256)
 
         def gather_vector(j, dst, j0, j1):
@@ -89,8 +88,9 @@ def tile_picked_idxput_max_e_kernel(tc, xT, mem, w1_words, w1_scales, offs, slot
             nc.vector.tensor_copy(out=dst, in_=rows.rearrange("p t s -> p s t"))
 
         def quantise(g, j0, j1):
+            codes = codes_first[:] if g == 0 else codes_second[j0 // RUN][:]
             nc.vector.quantize_mx(
-                out=codes[g][:, j0:j1].bitcast(FP8X4), scales=scales[g][:, j0:j1], in_=woven[g][:, j0:j1, :].rearrange("p s t -> p (s t)")
+                out=codes.bitcast(FP8X4), scales=scales[g][:, j0:j1], in_=woven[g][:, j0:j1, :].rearrange("p s t -> p (s t)")
             )
             for r in range(j0 // RUN, j1 // RUN):
                 cols = slice(r * RUN, (r + 1) * RUN)
@@ -98,7 +98,7 @@ def tile_picked_idxput_max_e_kernel(tc, xT, mem, w1_words, w1_scales, offs, slot
                     out=acc[r][:, :RUN],
                     lhsT=w_words[g][:].bitcast(FP4X4),
                     lhsT_scale=w_scales[:, g, :],
-                    rhs=codes[g][:, cols].bitcast(FP8X4),
+                    rhs=codes[:, r * RUN - j0 : (r + 1) * RUN - j0].bitcast(FP8X4),
                     rhs_scale=scales[g][:, cols],
                     start=(g == 0),
                     stop=(g == PASSES - 1),
@@ -140,12 +140,18 @@ def tile_picked_idxput_max_e_kernel(tc, xT, mem, w1_words, w1_scales, offs, slot
                 quantise(1, r * RUN, (r + 1) * RUN)
                 quantise(1, (r + 1) * RUN, (r + 2) * RUN)
 
-        nc.vector.tensor_copy(old[:, LOOK[0] : LOOK[1]], store[:].indirect(entries(slot_sb, *LOOK)))
-        for j0, j1 in ((0, RUN), (RUN, 2 * RUN), (2 * RUN, LOOK[0]), (LOOK[1], S)):
-            nc.scalar.activation(old[:, j0:j1], store[:].indirect(entries(slot_sb, j0, j1)), COPY)
-        for r in range(RUNS):
-            cols = slice(r * RUN, (r + 1) * RUN)
-            nc.vector.tensor_tensor(out=new[:, cols], in0=acc[r][:, :RUN], in1=old[:, cols], op=MAX)
+        old = {r: keep.tile([P, RUN], F32, name="old_%d" % r, align_bytes=256) for r in (0, 2, 3)}
+        for r in old:
+            nc.scalar.activation(old[r][:], store[:].indirect(entries(slot_sb, r * RUN, (r + 1) * RUN)), COPY)
+
+        def larger(r):
+            nc.vector.tensor_tensor(out=new[:, r * RUN : (r + 1) * RUN], in0=acc[r][:, :RUN], in1=old[r][:], op=MAX)
+
+        larger(0)
+        old[1] = keep.tile([P, RUN], F32, name="old_1", tag="codes_second_0", align_bytes=256)
+        nc.vector.tensor_copy(old[1][:], store[:].indirect(entries(slot_sb, RUN, 2 * RUN)))
+        for r in (2, 1, 3):
+            larger(r)
         for j0, j1 in ((0, RUN), (SPLIT, S)):
             nc.scalar.activation(fresh[:].indirect(entries(slot_sb, j0, j1)), new[:, j0:j1], COPY)
         nc.vector.tensor_copy(store[:].indirect(entries(slot_sb, RUN, SPLIT)), new[:, RUN:SPLIT])

from contextlib import ExitStack

import concourse.mybir as mybir

K, T, S, N, U = 1024, 2048, 1024, 128, 2048
FLOPS = 2 * K * N * S

F32 = mybir.dt.float32
BF16 = mybir.dt.bfloat16
U32 = mybir.dt.uint32
I32 = mybir.dt.int32
U16 = mybir.dt.uint16
U8 = mybir.dt.uint8
FP8X4 = mybir.dt.float8_e4m3fn_x4
FP4X4 = mybir.dt.float4_e2m1fn_x4
COPY = mybir.ActivationFunctionType.Copy
MAX = mybir.AluOpType.max
MULT = mybir.AluOpType.mult
ADD = mybir.AluOpType.add

P = 128
PASSES = 2
RUN = 256
RUNS = S // RUN
DIRECT = (512, 512, 256)
HALF = 640
LEAD = 128
POOLED = 256
CUTS = (0, 240, 560, 928, 1328, 1728, U)
SPLIT = 704
LOWEST = -(2.0**128 - 2.0**104)


def tile_picked_idxput_max_e_kernel(tc, xT, mem, w1_words, w1_scales, offs, slot, out):
    nc = tc.nc
    with ExitStack() as ctx:
        keep = ctx.enter_context(tc.tile_pool(name="keep", bufs=1))
        psum = ctx.enter_context(tc.psum_pool(name="psum", bufs=1))

        slot_sb = keep.tile([P, S // 16], U16, name="slot_sb")
        offs_sb = keep.tile([P, S // 16], U16, name="offs_sb")
        w_words = [keep.tile([P, 2 * N], U8, name="w_words_%d" % g, align_bytes=256) for g in range(PASSES)]
        w_scales = keep.tile([P, PASSES, N], U8, name="w_scales", align_bytes=256)
        store = keep.tile([P, U], F32, name="store", align_bytes=256)
        fresh = keep.tile([P, U], F32, name="fresh", align_bytes=256)
        lowest = keep.tile([P, 1], F32, name="lowest", align_bytes=256)

        x_rows = xT.rearrange("(g p t) c -> g t p c", g=PASSES, p=P, t=4)
        plane = [keep.tile([P, T], F32, name="plane_%d" % j, align_bytes=256) for j in range(8)]

        scale_rows = keep.tile([4, PASSES * 4, N], U8, name="scale_rows", align_bytes=256)
        nc.scalar.dma_start(out=scale_rows[:].bitcast(I32), in_=w1_scales.rearrange("g (q r) n -> r (g q) n", r=4).bitcast(I32))
        nc.scalar.dma_start(out=w_words[0][:].bitcast(I32), in_=w1_words[0].bitcast(I32))
        nc.sync.dma_start(out=plane[0][:], in_=x_rows[0, 0])
        nc.sync.dma_start(offs_sb[:], offs)
        for j in range(1, 8):
            nc.sync.dma_start(out=plane[j][:], in_=x_rows[j // 4, j % 4])
        nc.sync.dma_start(slot_sb[:], slot)
        nc.sync.dma_start(out=store[:], in_=mem)
        nc.sync.dma_start(out=w_words[1][:].bitcast(I32), in_=w1_words[1].bitcast(I32))

        nc.vector.memset(w_scales[:].rearrange("p g n -> p (g n)").bitcast(I32), 0)
        for q in range(4):
            nc.vector.tensor_copy(out=w_scales[32 * q : 32 * q + 4, :, :].bitcast(I32), in_=scale_rows[:, q::4, :].bitcast(I32))

        nc.vector.memset(lowest[:], LOWEST)
        nc.scalar.activation(fresh[:], lowest[:].to_broadcast([P, U]), COPY)

        def entries(lst, j0, j1):
            return lst[:, j0 // 16 : j1 // 16]

        woven = [keep.tile([P, S, 4], BF16, name="woven_%d" % g, align_bytes=256) for g in range(PASSES)]
        flat = [keep.tile([P, 2, S - DIRECT[h]], BF16, name="flat_%d" % h, align_bytes=256) for h in range(3)]
        last = keep.tile([P, 2, S - RUN], BF16, name="last", align_bytes=256)
        codes_first = keep.tile([P, S], U32, name="codes_first", align_bytes=256)
        codes_second = [keep.tile([P, RUN], U32, name="codes_second_%d" % r, tag="codes_second_%d" % r, align_bytes=256) for r in range(RUNS)]
        scales = [keep.tile([P, S], U8, name="scales_%d" % g, align_bytes=256) for g in range(PASSES)]
        acc = [psum.tile([P, 512], F32, name="acc_%d" % r) for r in range(RUNS)]
        new = keep.tile([P, S], F32, name="new", align_bytes=256)

        def gather_vector(j, dst, j0, j1):
            nc.vector.tensor_copy(dst, plane[j][:].indirect(entries(offs_sb, j0, j1)))

        def gather_scalar(j, dst, j0, j1):
            nc.scalar.activation(dst, plane[j][:].indirect(entries(offs_sb, j0, j1)), COPY)

        def weave(dst, rows):
            nc.vector.tensor_copy(out=dst, in_=rows.rearrange("p t s -> p s t"))

        def quantise(g, j0, j1):
            codes = codes_first[:] if g == 0 else codes_second[j0 // RUN][:]
            nc.vector.quantize_mx(
                out=codes.bitcast(FP8X4), scales=scales[g][:, j0:j1], in_=woven[g][:, j0:j1, :].rearrange("p s t -> p (s t)")
            )
            for r in range(j0 // RUN, j1 // RUN):
                cols = slice(r * RUN, (r + 1) * RUN)
                nc.tensor.matmul_mx(
                    out=acc[r][:, :RUN],
                    lhsT=w_words[g][:].bitcast(FP4X4),
                    lhsT_scale=w_scales[:, g, :],
                    rhs=codes[:, r * RUN - j0 : (r + 1) * RUN - j0].bitcast(FP8X4),
                    rhs_scale=scales[g][:, cols],
                    start=(g == 0),
                    stop=(g == PASSES - 1),
                )

        for j in range(4):
            gather_vector(j, woven[0][:, : DIRECT[0], j], 0, DIRECT[0])
            gather_scalar(j, flat[j // 2][:, j % 2, :POOLED], DIRECT[0], DIRECT[0] + POOLED)
            gather_scalar(j, flat[j // 2][:, j % 2, POOLED:], DIRECT[0] + POOLED, S)
            if j % 2 == 1:
                nc.gpsimd.tensor_scalar(
                    out=woven[0][:, DIRECT[0] : DIRECT[0] + POOLED, j - 1 : j + 1],
                    in0=flat[j // 2][:, :, :POOLED].rearrange("p t s -> p s t"),
                    scalar1=1.0,
                    scalar2=0.0,
                    op0=MULT,
                    op1=ADD,
                )
                weave(woven[0][:, DIRECT[0] + POOLED :, j - 1 : j + 1], flat[j // 2][:, :, POOLED:])
        gather_vector(4, woven[1][:, : DIRECT[2], 0], 0, DIRECT[2])
        gather_scalar(4, flat[2][:, 0, :], DIRECT[2], S)
        quantise(0, 0, S)
        gather_vector(5, woven[1][:, : DIRECT[2], 1], 0, DIRECT[2])
        for j0, j1 in ((DIRECT[2], HALF), (HALF, S)):
            gather_scalar(5, flat[2][:, 1, j0 - DIRECT[2] : j1 - DIRECT[2]], j0, j1)
            weave(woven[1][:, j0:j1, 0:2], flat[2][:, :, j0 - DIRECT[2] : j1 - DIRECT[2]])
        gather_vector(6, woven[1][:, LEAD : LEAD + RUN, 2], LEAD, LEAD + RUN)
        gather_scalar(6, last[:, 0, :LEAD], 0, LEAD)
        gather_scalar(6, last[:, 0, LEAD:], LEAD + RUN, S)
        gather_vector(7, woven[1][:, LEAD : LEAD + RUN, 3], LEAD, LEAD + RUN)
        pieces = ((LEAD + RUN, 2 * RUN), (2 * RUN, 3 * RUN), (3 * RUN, S))
        gather_scalar(7, last[:, 1, :LEAD], 0, LEAD)
        for j0, j1 in pieces:
            gather_scalar(7, last[:, 1, j0 - RUN : j1 - RUN], j0, j1)
        weave(woven[1][:, :LEAD, 2:4], last[:, :, :LEAD])
        for r, (j0, j1) in enumerate(pieces):
            weave(woven[1][:, j0:j1, 2:4], last[:, :, j0 - RUN : j1 - RUN])
            if r != 1:
                quantise(1, r * RUN, (r + 1) * RUN)
                quantise(1, (r + 1) * RUN, (r + 2) * RUN)

        old = {r: keep.tile([P, RUN], F32, name="old_%d" % r, align_bytes=256) for r in (0, 2, 3)}
        for r in old:
            nc.scalar.activation(old[r][:], store[:].indirect(entries(slot_sb, r * RUN, (r + 1) * RUN)), COPY)

        def larger(r):
            nc.vector.tensor_tensor(out=new[:, r * RUN : (r + 1) * RUN], in0=acc[r][:, :RUN], in1=old[r][:], op=MAX)

        larger(0)
        old[1] = keep.tile([P, RUN], F32, name="old_1", tag="codes_second_0", align_bytes=256)
        nc.vector.tensor_copy(old[1][:], store[:].indirect(entries(slot_sb, RUN, 2 * RUN)))
        for r in (2, 1, 3):
            larger(r)
        for j0, j1 in ((0, RUN), (SPLIT, S)):
            nc.scalar.activation(fresh[:].indirect(entries(slot_sb, j0, j1)), new[:, j0:j1], COPY)
        nc.vector.tensor_copy(store[:].indirect(entries(slot_sb, RUN, SPLIT)), new[:, RUN:SPLIT])

        for c0, c1 in zip(CUTS, CUTS[1:]):
            merged = keep.tile([P, c1 - c0], F32, name="merged_%d" % c0, align_bytes=256)
            nc.vector.tensor_tensor(out=merged[:], in0=fresh[:, c0:c1], in1=store[:, c0:c1], op=MAX)
            nc.sync.dma_start(out=out[:, c0:c1], in_=merged[:])
